import numpy as np
import ml_dtypes


def mxq(x, axis, fmt="e4m3"):
    dtype, down = {"e4m3": (ml_dtypes.float8_e4m3fn, 7), "e5m2": (ml_dtypes.float8_e5m2, 14)}[fmt]
    v = np.moveaxis(np.asarray(x, np.float32).astype(ml_dtypes.bfloat16).astype(np.float64), axis, -1)
    blocks = v.reshape(v.shape[:-1] + (-1, 32))
    amax = np.abs(blocks).max(-1, keepdims=True)
    byte = np.maximum(np.where(amax > 0, np.frexp(amax)[1] - 1 + 127, 0) - down, 1)
    scale = np.exp2(byte - 127.0)
    codes = (blocks / scale).astype(np.float32).astype(dtype).astype(np.float64)
    return np.moveaxis((codes * scale).reshape(v.shape), -1, axis)


WIDE = False


def mx_kscale(k):
    if not WIDE:
        return np.ones(k)
    levels = np.array([10, -10, 5, -5, 0])
    if k % 512:
        return np.exp2(np.random.permutation(np.resize(levels, k // 32))).repeat(32)
    a = np.empty((k // 512, 16))
    for p in range(k // 512):
        a[p, :8] = np.random.permutation(np.resize(levels, 8))
        for g in range(8):
            far = levels[np.abs(levels - a[p, g]) >= 10]
            a[p, g + 8] = far[np.random.randint(len(far))]
    return np.exp2(a.ravel()).repeat(32)


BF16 = ml_dtypes.bfloat16


def bf(x):
    return np.asarray(x, np.float32).astype(BF16)


def f64(x):
    return np.asarray(x).astype(np.float64)

def planes(Y):
    n, m = Y.shape
    b = f64(bf(Y)).reshape(n // 32, 32, m)
    amax = np.abs(b).max(1)
    byte = np.clip(np.where(amax > 0, np.frexp(amax)[1] - 1 + 127 - 7, 1), 1, 254)
    codes = (b * np.exp2(127.0 - byte)[:, None, :]).reshape(n, m).astype(np.float32).astype(ml_dtypes.float8_e4m3fn).view(np.uint8)
    words = codes.reshape(n // 512, 128, 4, m).transpose(0, 1, 3, 2)
    return np.ascontiguousarray(words), np.ascontiguousarray(byte.astype(np.uint8).reshape(n // 512, 16, m))


A, T, L, J = 4, 1024, 512, 512


def modulated_inputs(x, phase):
    return np.cos(phase)[:, :, None] * x[None, :, :]


def setup_inputs():
    s, r = mx_kscale(L), mx_kscale(T)
    x = np.random.standard_normal((T, L)) * s[None, :] * r[:, None]
    d = np.random.standard_normal((T, J)) * r[:, None]
    w = np.random.standard_normal((A, L, J)) * np.sqrt(2.0 / (A * L)) / s[None, :, None]
    phase = np.random.uniform(-3.14, 3.14, (A, T))
    v = (1.0 + 0.1 * np.random.standard_normal(T)) / (r * r)
    mu = np.random.uniform(0.05, 0.15, (A, L)) / np.sqrt(T) / (s * s)[None, :]
    return {"x": bf(x), "d": bf(d), "w": bf(w), "phase": bf(phase), "v": bf(v), "mu": bf(mu)}


def core(x, d, w, phase, v, mu):
    x, d, w, phase, v, mu = f64(x), f64(d), f64(w), f64(phase), f64(v), f64(mu)
    u = modulated_inputs(x, phase).transpose(1, 0, 2).reshape(T, A * L)
    est = mxq(u, 1, "e4m3") @ mxq(w.reshape(A * L, J), 0, "e4m3")
    err = (d - est) * v[:, None]
    g = (mxq(u, 0, "e4m3").T @ mxq(err, 0, "e4m3")).reshape(A, L, J)
    return w + mu[:, :, None] * g


def reference(x, d, w, phase, v, mu):
    R_out = core(x, d, w, phase, v, mu)
    words, scales = planes(np.moveaxis(R_out, 2, 0).reshape(512, -1))
    return R_out, words, scales

@@ -1,0 +1,372 @@
+import math
+from contextlib import ExitStack
+
+import concourse.mybir as mybir
+from concourse.masks import make_identity
+
+A, T, L, J = 4, 1024, 512, 512
+FLOPS = 2 * 2 * T * A * L * J
+
+F32 = mybir.dt.float32
+BF16 = mybir.dt.bfloat16
+U32 = mybir.dt.uint32
+I32 = mybir.dt.int32
+U8 = mybir.dt.uint8
+FP8X4 = mybir.dt.float8_e4m3fn_x4
+ALU = mybir.AluOpType
+ACT = mybir.ActivationFunctionType
+
+P = 128
+PACK = 4
+G = T // (P * PACK)
+PAD = 16
+
+
+def tile_freshcyclicfilterblocklmsupdate_x1_kernel(tc, x, d, w, phase, v, mu, out_0, out_1, out_2):
+    nc = tc.nc
+    with ExitStack() as ctx:
+        keep = ctx.enter_context(tc.tile_pool(name="keep", bufs=1))
+        stage = ctx.enter_context(tc.tile_pool(name="stage", bufs=3))
+        psum = ctx.enter_context(tc.psum_pool(name="psum", bufs=1))
+        ctx.enter_context(tc.manual_schedule())
+
+        def kept(name, shape, dtype):
+            return keep.tile(shape, dtype, name=name, align_bytes=64)
+
+        def staged(tag, name, shape, dtype):
+            return stage.tile(shape, dtype, name=name, tag=tag, align_bytes=64)
+
+        def bank(number, name, shape):
+            return psum.tile(shape, F32, name=name, tag="bank%d" % number)
+
+        def copy_on(engine, out, in_):
+            if engine == "vector":
+                nc.vector.tensor_copy(out=out, in_=in_)
+            else:
+                nc.scalar.copy(out=out, in_=in_)
+
+        def quantize(name, grouped, tag=None):
+            if tag is None:
+                codes = kept(name + "_codes", [P, 512], U32)
+                scales = kept(name + "_scales", [P, 512], U8)
+            else:
+                codes = staged(tag + "_codes", name + "_codes", [P, 512], U32)
+                scales = staged(tag + "_scales", name + "_scales", [P, 512], U8)
+            nc.vector.quantize_mx(
+                out=codes[:].bitcast(FP8X4), scales=scales[:], in_=grouped[:].rearrange("p c i -> p (c i)")
+            )
+            return codes, scales
+
+        def interleave(engine, grouped, rows, first, last):
+            copy_on(
+                engine,
+                grouped[:, first:last, :].rearrange("p (c r) i -> p c i r", r=4),
+                rows[:, :, first:last].rearrange("p i (c r) -> p c i r", r=4),
+            )
+
+        phase_sb = kept("phase_sb", [P, A * G, PAD], BF16)
+        v_sb = kept("v_sb", [P, G, PAD], BF16)
+        mu_sb = kept("mu_sb", [P, A, PAD], BF16)
+        x_rows = [kept("x_rows%d" % g, [P, PACK, L], BF16) for g in range(G)]
+        d_rows = [kept("d_rows%d" % g, [P, PACK, J], BF16) for g in range(G)]
+        w_rows = [kept("w_rows%d" % a, [P, PACK, J], BF16) for a in range(A)]
+
+        def load_rows(dst, src):
+            nc.sync.dma_start(out=dst[:], in_=src.rearrange("(p i) c -> p i c", i=PACK))
+
+        nc.sync.dma_start(out=phase_sb[:, :, 0:PACK], in_=phase.rearrange("a (g p i) -> p (a g) i", g=G, i=PACK))
+        load_rows(x_rows[0], x[0:512, :])
+        load_rows(w_rows[0], w[0])
+        load_rows(w_rows[1], w[1])
+        load_rows(x_rows[1], x[512:1024, :])
+        load_rows(w_rows[2], w[2])
+        nc.sync.dma_start(out=v_sb[:, :, 0:PACK], in_=v.rearrange("(g p i) -> p g i", g=G, i=PACK))
+        load_rows(w_rows[3], w[3])
+        load_rows(d_rows[0], d[0:512, :])
+        load_rows(d_rows[1], d[512:1024, :])
+        nc.sync.dma_start(out=mu_sb[:, :, 0:PACK], in_=mu.rearrange("a (q i) -> q a i", i=PACK))
+
+        ident = kept("ident", [P, P], F32)
+        make_identity(nc, ident[:])
+        warm_in = kept("warm_in", [P, 1], F32)
+        warm_out = kept("warm_out", [P, 1], F32)
+        nc.vector.memset(warm_in[:], 0.0)
+        nc.scalar.activation(out=warm_out[:], in_=warm_in[:], func=ACT.Sin)
+
+        neg_abs = kept("neg_abs", [P, A * G, PACK], F32)
+        cos_sb = kept("cos_sb", [P, A * G, PACK], F32)
+        neg_v = kept("neg_v", [P, G, PACK], F32)
+        x_perm = [kept("x_perm%d" % g, [P, PACK, L], BF16) for g in range(G)]
+        u_rows = {}
+        u1_banks, u1_grouped, u1_q = {}, {}, {}
+        w_grouped, w_q = {}, {}
+        est = {}
+        d_neg_v = {}
+        err_rows = [kept("err_rows%d" % g, [P, PACK, J], BF16) for g in range(G)]
+        err_grouped = [kept("err_grouped%d" % g, [P, J, PACK], BF16) for g in range(G)]
+        err_q = {}
+        u2_grouped, u2_q = {}, {}
+        grad = {}
+        result = [kept("result%d" % a, [P, PACK, J], F32) for a in range(A)]
+        result_bf, plane_banks, plane_grouped = {}, {}, {}
+        plane_scales = kept("plane_scales", [P, A * L], U8)
+
+        def cosine():
+            nc.vector.scalar_tensor_tensor(
+                out=neg_abs[:], in0=phase_sb[:, :, 0:PACK], scalar=-1.0, in1=phase_sb[:, :, 0:PACK],
+                op0=ALU.mult, op1=ALU.min,
+            )
+            nc.scalar.activation(out=cos_sb[:], in_=neg_abs[:], func=ACT.Sin, bias=math.pi / 2)
+
+        def negate_v():
+            nc.vector.tensor_scalar(out=neg_v[:], in0=v_sb[:, :, 0:PACK], scalar1=-1.0, scalar2=None, op0=ALU.mult)
+
+        def permute_x(engine, g):
+            src = x_rows[g][:].rearrange("p i l -> p (i l)").bitcast(F32)
+            dst = x_perm[g][:].rearrange("p i l -> p (i l)").bitcast(F32)
+            copy_on(engine, dst.rearrange("p (i u q) -> p i u q", i=PACK, u=2), src.rearrange("p (i q u) -> p i u q", i=PACK, u=2))
+
+        def modulate(g, a):
+            u_rows[g, a] = kept("u_rows%d%d" % (g, a), [P, PACK, L], BF16)
+            for i in range(PACK):
+                nc.vector.tensor_scalar(
+                    out=u_rows[g, a][:, i, :], in0=x_perm[g][:, i, :],
+                    scalar1=cos_sb[:, a * G + g, i : i + 1], scalar2=None, op0=ALU.mult,
+                )
+
+        def turn(rows, half, dst):
+            words = rows[:].rearrange("p i c -> p (i c)").bitcast(F32)
+            for n in range(4):
+                first = (4 * half + n) * P
+                nc.tensor.transpose(dst[:, n, :], words[:, first : first + P], ident[:])
+
+        def turn_u(g, a):
+            for half in range(2):
+                u1_banks[g, a, half] = bank(2 * (a % 2) + half, "u1_bank%d%d%d" % (g, a, half), [P, 4, P])
+                turn(u_rows[g, a], half, u1_banks[g, a, half])
+
+        def gather_u1(engine, g, a, half):
+            if (g, a) not in u1_grouped:
+                u1_grouped[g, a] = staged("u1_grouped", "u1_grouped%d%d" % (g, a), [P, 512, PACK], BF16)
+            words = u1_grouped[g, a][:, 256 * half : 256 * (half + 1), :].rearrange("q c k -> q (c k)").bitcast(F32)
+            copy_on(
+                engine,
+                words.rearrange("q (i p u) -> q i p u", i=2, u=2),
+                u1_banks[g, a, half][:].rearrange("q (i u) p -> q i p u", u=2),
+            )
+
+        def quantize_u1(g, a):
+            u1_q[g, a] = quantize("u1_%d%d" % (g, a), u1_grouped[g, a], "u1")
+
+        def group_w(engine, a, first, last):
+            if a not in w_grouped:
+                w_grouped[a] = staged("plane_grouped", "w_grouped%d" % a, [P, J, PACK], BF16)
+            interleave(engine, w_grouped[a], w_rows[a], first, last)
+
+        def quantize_w(a):
+            w_q[a] = quantize("w_%d" % a, w_grouped[a])
+
+        def mx_pass(acc, stationary, i, moving, start, stop):
+            cols = slice(i * P, (i + 1) * P)
+            nc.tensor.matmul_mx(
+                out=acc[:], lhsT=stationary[0][:, cols].bitcast(FP8X4), lhsT_scale=stationary[1][:, cols],
+                rhs=moving[0][:].bitcast(FP8X4), rhs_scale=moving[1][:], start=start, stop=stop,
+            )
+
+        def estimate(g, a):
+            for i in range(PACK):
+                if a == 0:
+                    est[g, i] = bank(4 + i, "est%d%d" % (g, i), [P, J])
+                mx_pass(est[g, i], u1_q[g, a], i, w_q[a], a == 0, a == A - 1)
+
+        def weight_d(g, i):
+            if i == 0:
+                d_neg_v[g] = keep.tile([P, PACK, J], F32, name="d_neg_v%d" % g, tag="d_neg_v", align_bytes=64)
+            nc.scalar.activation(
+                out=d_neg_v[g][:, i, :], in_=d_rows[g][:, i, :], func=ACT.Copy, scale=neg_v[:, g, i : i + 1]
+            )
+
+        def error(g, i):
+            nc.vector.scalar_tensor_tensor(
+                out=err_rows[g][:, i, :], in0=est[g, i][:], scalar=neg_v[:, g, i : i + 1], in1=d_neg_v[g][:, i, :],
+                op0=ALU.mult, op1=ALU.subtract,
+            )
+
+        def group_err(engine, g, first, last):
+            interleave(engine, err_grouped[g], err_rows[g], first, last)
+
+        def quantize_err(g):
+            err_q[g] = quantize("err_%d" % g, err_grouped[g])
+
+        def group_u2(engine, g, a, u):
+            if (g, a) not in u2_grouped:
+                u2_grouped[g, a] = staged("u2_grouped", "u2_grouped%d%d" % (g, a), [P, L, PACK], BF16)
+            cols = slice(256 * u, 256 * (u + 1))
+            copy_on(
+                engine,
+                u2_grouped[g, a][:, cols, :].rearrange("p (e c r) i -> p c i r e", e=2, r=2),
+                u_rows[g, a][:, :, cols].rearrange("p i (c r e) -> p c i r e", r=2, e=2),
+            )
+
+        def quantize_u2(g, a):
+            u2_q[g, a] = quantize("u2_%d%d" % (g, a), u2_grouped[g, a])
+
+        def gradient(g, a, i):
+            if g == 0:
+                grad[a, i] = bank((PACK * a + i) % 6, "grad%d%d" % (a, i), [P, J])
+            mx_pass(grad[a, i], u2_q[g, a], i, err_q[g], g == 0, g == G - 1)
+
+        def update(a, i):
+            nc.vector.scalar_tensor_tensor(
+                out=result[a][:, i, :], in0=grad[a, i][:], scalar=mu_sb[:, a, i : i + 1], in1=w_rows[a][:, i, :],
+                op0=ALU.mult, op1=ALU.add,
+            )
+
+        def store_result(a, first, last):
+            nc.sync.dma_start(
+                out=out_0[a].rearrange("(q i) j -> q i j", i=PACK)[:, first:last, :], in_=result[a][:, first:last, :]
+            )
+
+        def round_result(engine, a, i):
+            if a not in result_bf:
+                result_bf[a] = staged("result_bf", "result_bf%d" % a, [P, PACK, J], BF16)
+            dst = result_bf[a][:, i, :].rearrange("q (u p e) -> q u p e", u=2, e=2)
+            src = result[a][:, i, :].rearrange("q (p u e) -> q u p e", u=2, e=2)
+            if engine == "gpsimd":
+                nc.gpsimd.tensor_scalar(out=dst, in0=src, scalar1=1.0, scalar2=0.0, op0=ALU.mult, op1=ALU.add)
+            else:
+                copy_on(engine, dst, src)
+
+        def turn_result(a, half):
+            plane_banks[a, half] = bank(6 + half, "plane_bank%d%d" % (a, half), [P, 4, P])
+            turn(result_bf[a], half, plane_banks[a, half])
+
+        def gather_plane(engine, a, half):
+            if a not in plane_grouped:
+                plane_grouped[a] = staged("plane_grouped", "plane_grouped%d" % a, [P, L, PACK], BF16)
+            words = plane_grouped[a][:].rearrange("p m k -> p (m k)").bitcast(F32)
+            copy_on(
+                engine,
+                words.rearrange("p (q i u) -> p q i u", i=PACK, u=2)[:, :, 2 * half : 2 * half + 2, :],
+                plane_banks[a, half][:].rearrange("p (i u) q -> p q i u", u=2),
+            )
+
+        def quantize_plane(a):
+            cols = slice(a * L, (a + 1) * L)
+            codes = kept("plane_codes%d" % a, [P, L], U32)
+            nc.vector.quantize_mx(
+                out=codes[:].bitcast(FP8X4), scales=plane_scales[:, cols],
+                in_=plane_grouped[a][:].rearrange("p m k -> p (m k)"),
+            )
+            words = out_1.rearrange("g p m k -> (g p) (m k)").bitcast(I32)
+            nc.sync.dma_start(out=words[:, cols], in_=codes[:].bitcast(I32))
+
+        def store_scales():
+            for quad in range(4):
+                queue = nc.sync if quad % 2 == 0 else nc.scalar
+                queue.dma_start(
+                    out=out_2[0, 4 * quad : 4 * quad + 4, :].bitcast(I32),
+                    in_=plane_scales[32 * quad : 32 * quad + 4, :].bitcast(I32),
+                )
+
+        V, S = "vector", "scalar"
+        steps = [(g, a) for g in range(G) for a in range(A)]
+        cosine()
+        permute_x(V, 0)
+        modulate(0, 0)
+        turn_u(0, 0)
+        group_w(S, 0, 256, 512)
+        modulate(0, 1)
+        turn_u(0, 1)
+        group_w(V, 0, 0, 256)
+        permute_x(V, 1)
+        quantize_w(0)
+        for k, (g, a) in enumerate(steps):
+            gather_u1(S, g, a, 0)
+            gather_u1(S, g, a, 1)
+            if k + 2 < len(steps):
+                modulate(*steps[k + 2])
+                turn_u(*steps[k + 2])
+            if k + 1 < A:
+                group_w(S, k + 1, 224, 512)
+                group_w(V, k + 1, 0, 224)
+            if k == 2:
+                negate_v()
+            if k == 3:
+                for i in range(PACK):
+                    weight_d(0, i)
+                group_u2(V, 0, 0, 0)
+                group_u2(V, 0, 0, 1)
+            quantize_u1(g, a)
+            if k + 1 < A:
+                quantize_w(k + 1)
+            if k == 4:
+                for i in range(PACK):
+                    error(0, i)
+                group_u2(S, 0, 1, 0)
+                group_u2(S, 0, 1, 1)
+                quantize_u2(0, 0)
+            estimate(g, a)
+            if k == 5:
+                group_err(S, 0, 256, 512)
+                group_err(V, 0, 0, 256)
+                quantize_u2(0, 1)
+                group_u2(V, 1, 0, 0)
+            if k == 6:
+                group_u2(V, 1, 0, 1)
+                quantize_err(0)
+                for i in range(PACK):
+                    weight_d(1, i)
+                quantize_u2(1, 0)
+                group_u2(V, 1, 1, 0)
+        group_u2(S, 1, 1, 1)
+        group_u2(V, 0, 2, 0)
+        group_u2(S, 0, 2, 1)
+        group_u2(S, 1, 2, 0)
+        for i in range(PACK):
+            gradient(0, 0, i)
+        for i in range(PACK):
+            error(1, i)
+        quantize_u2(1, 1)
+        group_err(S, 1, 352, 512)
+        group_err(V, 1, 0, 352)
+        quantize_u2(0, 2)
+        group_u2(S, 1, 2, 1)
+        quantize_err(1)
+        for i in range(PACK):
+            gradient(1, 0, i)
+        for i in range(2):
+            gradient(0, 1, i)
+            gradient(1, 1, i)
+        quantize_u2(1, 2)
+        group_u2(S, 0, 3, 0)
+        group_u2(S, 0, 3, 1)
+        group_u2(S, 1, 3, 0)
+        group_u2(S, 1, 3, 1)
+        tiles = [(a, i) for a in range(A) for i in range(PACK)]
+        for n in range(len(tiles) + 3):
+            if n < len(tiles):
+                a, i = tiles[n]
+                update(a, i)
+                if i % 2 == 1:
+                    store_result(a, i - 1, i + 1)
+            if n == 3:
+                quantize_u2(0, 3)
+            if n == 5:
+                quantize_u2(1, 3)
+            if 1 <= n <= len(tiles):
+                pa, pi = tiles[n - 1]
+                round_result(V if (n - 1 < 6 or n - 1 in (9, 13, 15)) else S, pa, pi)
+                if pi % 2 == 1:
+                    turn_result(pa, pi // 2)
+            if n + 6 < len(tiles):
+                gradient(0, *tiles[n + 6])
+                gradient(1, *tiles[n + 6])
+            if 2 <= n - 1 <= len(tiles) + 1:
+                pa, pi = tiles[n - 3]
+                if pi % 2 == 1:
+                    gather_plane(S, pa, pi // 2)
+            if n >= 8 and n % 4 == 0:
+                quantize_plane(n // 4 - 2)
+        quantize_plane(A - 1)
+        store_scales()

@@ -74,8 +74,10 @@ def tile_freshcyclicfilterblocklmsupdate_x1_kernel(tc, x, d, w, phase, v, mu, ou
         def load_rows(dst, src):
             nc.sync.dma_start(out=dst[:], in_=src.rearrange("(p i) c -> p i c", i=PACK))
 
-        nc.sync.dma_start(out=phase_sb[:, :, 0:PACK], in_=phase.rearrange("a (g p i) -> p (a g) i", g=G, i=PACK))
-        load_rows(x_rows[0], x[0:512, :])
+        nc.scalar.dma_start(out=phase_sb[:, :, 0:PACK], in_=phase.rearrange("a (g p i) -> p (a g) i", g=G, i=PACK))
+        x_first = x[0:512, :].rearrange("(p i) c -> p i c", i=PACK)
+        nc.sync.dma_start(out=x_rows[0][:, 0:2, :], in_=x_first[:, 0:2, :])
+        nc.sync.dma_start(out=x_rows[0][:, 2:4, :], in_=x_first[:, 2:4, :])
         load_rows(w_rows[0], w[0])
         load_rows(w_rows[1], w[1])
         load_rows(x_rows[1], x[512:1024, :])
@@ -95,13 +97,12 @@ def tile_freshcyclicfilterblocklmsupdate_x1_kernel(tc, x, d, w, phase, v, mu, ou
 
         neg_abs = kept("neg_abs", [P, A * G, PACK], F32)
         cos_sb = kept("cos_sb", [P, A * G, PACK], F32)
-        neg_v = kept("neg_v", [P, G, PACK], F32)
-        x_perm = [kept("x_perm%d" % g, [P, PACK, L], BF16) for g in range(G)]
+        v_f32 = kept("v_f32", [P, G, PACK], F32)
         u_rows = {}
         u1_banks, u1_grouped, u1_q = {}, {}, {}
         w_grouped, w_q = {}, {}
         est = {}
-        d_neg_v = {}
+        diff = {}
         err_rows = [kept("err_rows%d" % g, [P, PACK, J], BF16) for g in range(G)]
         err_grouped = [kept("err_grouped%d" % g, [P, J, PACK], BF16) for g in range(G)]
         err_q = {}
@@ -109,6 +110,7 @@ def tile_freshcyclicfilterblocklmsupdate_x1_kernel(tc, x, d, w, phase, v, mu, ou
         grad = {}
         result = [kept("result%d" % a, [P, PACK, J], F32) for a in range(A)]
         result_bf, plane_banks, plane_grouped = {}, {}, {}
+        plane_codes = kept("plane_codes", [P, A * L], U32)
         plane_scales = kept("plane_scales", [P, A * L], U8)
 
         def cosine():
@@ -118,32 +120,26 @@ def tile_freshcyclicfilterblocklmsupdate_x1_kernel(tc, x, d, w, phase, v, mu, ou
             )
             nc.scalar.activation(out=cos_sb[:], in_=neg_abs[:], func=ACT.Sin, bias=math.pi / 2)
 
-        def negate_v():
-            nc.vector.tensor_scalar(out=neg_v[:], in0=v_sb[:, :, 0:PACK], scalar1=-1.0, scalar2=None, op0=ALU.mult)
-
-        def permute_x(engine, g):
-            src = x_rows[g][:].rearrange("p i l -> p (i l)").bitcast(F32)
-            dst = x_perm[g][:].rearrange("p i l -> p (i l)").bitcast(F32)
-            copy_on(engine, dst.rearrange("p (i u q) -> p i u q", i=PACK, u=2), src.rearrange("p (i q u) -> p i u q", i=PACK, u=2))
+        def widen_v():
+            nc.vector.tensor_copy(out=v_f32[:], in_=v_sb[:, :, 0:PACK])
 
         def modulate(g, a):
             u_rows[g, a] = kept("u_rows%d%d" % (g, a), [P, PACK, L], BF16)
             for i in range(PACK):
                 nc.vector.tensor_scalar(
-                    out=u_rows[g, a][:, i, :], in0=x_perm[g][:, i, :],
+                    out=u_rows[g, a][:, i, :], in0=x_rows[g][:, i, :],
                     scalar1=cos_sb[:, a * G + g, i : i + 1], scalar2=None, op0=ALU.mult,
                 )
 
-        def turn(rows, half, dst):
-            words = rows[:].rearrange("p i c -> p (i c)").bitcast(F32)
-            for n in range(4):
-                first = (4 * half + n) * P
-                nc.tensor.transpose(dst[:, n, :], words[:, first : first + P], ident[:])
-
-        def turn_u(g, a):
-            for half in range(2):
+        def turn_u(g, a, half):
+            if True:
                 u1_banks[g, a, half] = bank(2 * (a % 2) + half, "u1_bank%d%d%d" % (g, a, half), [P, 4, P])
-                turn(u_rows[g, a], half, u1_banks[g, a, half])
+                words = u_rows[g, a][:].rearrange("p i l -> p (i l)").bitcast(F32)
+                for n in range(4):
+                    i, u = 2 * half + n // 2, n % 2
+                    nc.tensor.transpose(
+                        u1_banks[g, a, half][:, n, :], words[:, 256 * i + u : 256 * (i + 1) : 2], ident[:]
+                    )
 
         def gather_u1(engine, g, a, half):
             if (g, a) not in u1_grouped:
@@ -155,8 +151,16 @@ def tile_freshcyclicfilterblocklmsupdate_x1_kernel(tc, x, d, w, phase, v, mu, ou
                 u1_banks[g, a, half][:].rearrange("q (i u) p -> q i p u", u=2),
             )
 
-        def quantize_u1(g, a):
-            u1_q[g, a] = quantize("u1_%d%d" % (g, a), u1_grouped[g, a], "u1")
+        def quantize_u1(g, a, half):
+            if half == 0:
+                codes = staged("u1_codes", "u1_codes%d%d" % (g, a), [P, 512], U32)
+                scales = staged("u1_scales", "u1_scales%d%d" % (g, a), [P, 512], U8)
+                u1_q[g, a] = codes, scales
+            cols = slice(256 * half, 256 * (half + 1))
+            nc.vector.quantize_mx(
+                out=u1_q[g, a][0][:, cols].bitcast(FP8X4), scales=u1_q[g, a][1][:, cols],
+                in_=u1_grouped[g, a][:, cols, :].rearrange("p c i -> p (c i)"),
+            )
 
         def group_w(engine, a, first, last):
             if a not in w_grouped:
@@ -173,24 +177,25 @@ def tile_freshcyclicfilterblocklmsupdate_x1_kernel(tc, x, d, w, phase, v, mu, ou
                 rhs=moving[0][:].bitcast(FP8X4), rhs_scale=moving[1][:], start=start, stop=stop,
             )
 
-        def estimate(g, a):
-            for i in range(PACK):
+        def estimate(g, a, half):
+            for i in range(2 * half, 2 * half + 2):
                 if a == 0:
                     est[g, i] = bank(4 + i, "est%d%d" % (g, i), [P, J])
                 mx_pass(est[g, i], u1_q[g, a], i, w_q[a], a == 0, a == A - 1)
 
-        def weight_d(g, i):
+        def subtract_estimate(g, i):
             if i == 0:
-                d_neg_v[g] = keep.tile([P, PACK, J], F32, name="d_neg_v%d" % g, tag="d_neg_v", align_bytes=64)
-            nc.scalar.activation(
-                out=d_neg_v[g][:, i, :], in_=d_rows[g][:, i, :], func=ACT.Copy, scale=neg_v[:, g, i : i + 1]
-            )
+                diff[g] = keep.tile([P, PACK, J], F32, name="diff%d" % g, tag="diff", align_bytes=64)
+            nc.vector.tensor_tensor(out=diff[g][:, i, :], in0=d_rows[g][:, i, :], in1=est[g, i][:], op=ALU.subtract)
 
-        def error(g, i):
-            nc.vector.scalar_tensor_tensor(
-                out=err_rows[g][:, i, :], in0=est[g, i][:], scalar=neg_v[:, g, i : i + 1], in1=d_neg_v[g][:, i, :],
-                op0=ALU.mult, op1=ALU.subtract,
-            )
+        def weight_error(engine, g, i):
+            dst, src, factor = err_rows[g][:, i, :], diff[g][:, i, :], v_f32[:, g, i : i + 1]
+            if engine == "gpsimd":
+                nc.gpsimd.tensor_scalar(out=dst, in0=src, scalar1=factor, scalar2=0.0, op0=ALU.mult, op1=ALU.add)
+            elif engine == "vector":
+                nc.vector.tensor_scalar(out=dst, in0=src, scalar1=factor, scalar2=None, op0=ALU.mult)
+            else:
+                nc.scalar.activation(out=dst, in_=src, func=ACT.Copy, scale=factor)
 
         def group_err(engine, g, first, last):
             interleave(engine, err_grouped[g], err_rows[g], first, last)
@@ -205,7 +210,7 @@ def tile_freshcyclicfilterblocklmsupdate_x1_kernel(tc, x, d, w, phase, v, mu, ou
             copy_on(
                 engine,
                 u2_grouped[g, a][:, cols, :].rearrange("p (e c r) i -> p c i r e", e=2, r=2),
-                u_rows[g, a][:, :, cols].rearrange("p i (c r e) -> p c i r e", r=2, e=2),
+                u_rows[g, a][:].rearrange("p i (c r u e) -> p c i r u e", r=2, u=2, e=2)[:, :, :, :, u, :],
             )
 
         def quantize_u2(g, a):
@@ -237,29 +242,39 @@ def tile_freshcyclicfilterblocklmsupdate_x1_kernel(tc, x, d, w, phase, v, mu, ou
             else:
                 copy_on(engine, dst, src)
 
-        def turn_result(a, half):
-            plane_banks[a, half] = bank(6 + half, "plane_bank%d%d" % (a, half), [P, 4, P])
-            turn(result_bf[a], half, plane_banks[a, half])
+        def update_rounded(a, i):
+            nc.vector.scalar_tensor_tensor(
+                out=result_bf[a][:, i, :], in0=grad[a, i][:], scalar=mu_sb[:, a, i : i + 1], in1=w_rows[a][:, i, :],
+                op0=ALU.mult, op1=ALU.add,
+            )
 
-        def gather_plane(engine, a, half):
+        def turn_result(a, i, natural=False):
+            half = i // 2
+            if i % 2 == 0:
+                plane_banks[a, half] = bank((6 if a < A - 1 else 4) + half, "plane_bank%d%d" % (a, half), [P, 4, P])
+            words = result_bf[a][:, i, :].bitcast(F32)
+            for u in range(2):
+                src = words[:, u:256:2] if natural else words[:, u * P : (u + 1) * P]
+                nc.tensor.transpose(plane_banks[a, half][:, 2 * (i % 2) + u, :], src, ident[:])
+
+        def gather_plane(engine, a, half, first=0, last=P):
             if a not in plane_grouped:
                 plane_grouped[a] = staged("plane_grouped", "plane_grouped%d" % a, [P, L, PACK], BF16)
             words = plane_grouped[a][:].rearrange("p m k -> p (m k)").bitcast(F32)
             copy_on(
                 engine,
-                words.rearrange("p (q i u) -> p q i u", i=PACK, u=2)[:, :, 2 * half : 2 * half + 2, :],
-                plane_banks[a, half][:].rearrange("p (i u) q -> p q i u", u=2),
+                words.rearrange("p (q i u) -> p q i u", i=PACK, u=2)[:, first:last, 2 * half : 2 * half + 2, :],
+                plane_banks[a, half][:].rearrange("p (i u) q -> p q i u", u=2)[:, first:last],
             )
 
-        def quantize_plane(a):
-            cols = slice(a * L, (a + 1) * L)
-            codes = kept("plane_codes%d" % a, [P, L], U32)
+        def quantize_plane(a, first=0, last=L):
+            cols = slice(a * L + first, a * L + last)
             nc.vector.quantize_mx(
-                out=codes[:].bitcast(FP8X4), scales=plane_scales[:, cols],
-                in_=plane_grouped[a][:].rearrange("p m k -> p (m k)"),
+                out=plane_codes[:, cols].bitcast(FP8X4), scales=plane_scales[:, cols],
+                in_=plane_grouped[a][:, first:last, :].rearrange("p m k -> p (m k)"),
             )
             words = out_1.rearrange("g p m k -> (g p) (m k)").bitcast(I32)
-            nc.sync.dma_start(out=words[:, cols], in_=codes[:].bitcast(I32))
+            nc.sync.dma_start(out=words[:, cols], in_=plane_codes[:, cols].bitcast(I32))
 
         def store_scales():
             for quad in range(4):
@@ -269,68 +284,107 @@ def tile_freshcyclicfilterblocklmsupdate_x1_kernel(tc, x, d, w, phase, v, mu, ou
                     in_=plane_scales[32 * quad : 32 * quad + 4, :].bitcast(I32),
                 )
 
-        V, S = "vector", "scalar"
+        V, S, Q = "vector", "scalar", "gpsimd"
         steps = [(g, a) for g in range(G) for a in range(A)]
+
+        def modulate_and_turn(k):
+            modulate(*steps[k])
+            turn_u(*steps[k], 0)
+            turn_u(*steps[k], 1)
+
+        def gather(k):
+            gather_u1(S, *steps[k], 0)
+            gather_u1(S, *steps[k], 1)
+
+        def stage_one(k):
+            for half in range(2):
+                quantize_u1(*steps[k], half)
+                estimate(*steps[k], half)
+
         cosine()
-        permute_x(V, 0)
-        modulate(0, 0)
-        turn_u(0, 0)
-        group_w(S, 0, 256, 512)
-        modulate(0, 1)
-        turn_u(0, 1)
-        group_w(V, 0, 0, 256)
-        permute_x(V, 1)
+        modulate_and_turn(0)
+        group_u2(S, 0, 0, 0)
+        modulate_and_turn(1)
+        modulate(*steps[2])
+        group_w(V, 0, 0, 512)
+        gather(0)
+        turn_u(*steps[2], 0)
+        turn_u(*steps[2], 1)
+        modulate(*steps[3])
+        group_u2(S, 0, 0, 1)
         quantize_w(0)
-        for k, (g, a) in enumerate(steps):
-            gather_u1(S, g, a, 0)
-            gather_u1(S, g, a, 1)
-            if k + 2 < len(steps):
-                modulate(*steps[k + 2])
-                turn_u(*steps[k + 2])
-            if k + 1 < A:
-                group_w(S, k + 1, 224, 512)
-                group_w(V, k + 1, 0, 224)
-            if k == 2:
-                negate_v()
-            if k == 3:
-                for i in range(PACK):
-                    weight_d(0, i)
-                group_u2(V, 0, 0, 0)
-                group_u2(V, 0, 0, 1)
-            quantize_u1(g, a)
-            if k + 1 < A:
-                quantize_w(k + 1)
-            if k == 4:
-                for i in range(PACK):
-                    error(0, i)
-                group_u2(S, 0, 1, 0)
-                group_u2(S, 0, 1, 1)
-                quantize_u2(0, 0)
-            estimate(g, a)
-            if k == 5:
-                group_err(S, 0, 256, 512)
-                group_err(V, 0, 0, 256)
-                quantize_u2(0, 1)
-                group_u2(V, 1, 0, 0)
-            if k == 6:
-                group_u2(V, 1, 0, 1)
-                quantize_err(0)
-                for i in range(PACK):
-                    weight_d(1, i)
-                quantize_u2(1, 0)
-                group_u2(V, 1, 1, 0)
-        group_u2(S, 1, 1, 1)
-        group_u2(V, 0, 2, 0)
+        group_w(V, 1, 0, 512)
+        stage_one(0)
+        gather(1)
+        turn_u(*steps[3], 0)
+        turn_u(*steps[3], 1)
+        group_w(S, 2, 192, 512)
+        quantize_w(1)
+        group_w(V, 2, 0, 192)
+        modulate(*steps[4])
+        stage_one(1)
+        gather(2)
+        turn_u(*steps[4], 0)
+        turn_u(*steps[4], 1)
+        group_w(S, 3, 0, 512)
+        quantize_u2(0, 0)
+        quantize_w(2)
+        modulate(*steps[5])
+        stage_one(2)
+        gather(3)
+        turn_u(*steps[5], 0)
+        turn_u(*steps[5], 1)
+        group_u2(S, 1, 0, 0)
+        modulate(*steps[6])
+        group_u2(V, 0, 1, 0)
+        quantize_w(3)
+        stage_one(3)
+        gather(4)
+        turn_u(*steps[6], 0)
+        turn_u(*steps[6], 1)
+        group_u2(S, 1, 0, 1)
+        modulate(*steps[7])
+        group_u2(V, 0, 1, 1)
+        widen_v()
+        quantize_u1(*steps[4], 0)
+        quantize_u1(*steps[4], 1)
+        gather(5)
+        turn_u(*steps[7], 0)
+        turn_u(*steps[7], 1)
+        group_u2(S, 1, 1, 0)
+        quantize_u2(0, 1)
+        for i in range(PACK):
+            subtract_estimate(0, i)
+            if i < 2:
+                weight_error(Q, 0, i)
+        estimate(*steps[4], 0)
+        estimate(*steps[4], 1)
+        gather(6)
+        stage_one(5)
+        gather(7)
+        quantize_u2(1, 0)
+        stage_one(6)
+        weight_error(S, 0, 2)
+        weight_error(S, 0, 3)
+        group_u2(V, 1, 1, 1)
+        stage_one(7)
+        group_u2(S, 0, 2, 0)
+        group_err(S, 0, 96, 512)
+        group_err(V, 0, 0, 96)
+        quantize_u2(1, 1)
+        for i in range(PACK):
+            subtract_estimate(1, i)
+            if i < 2:
+                weight_error(Q, 1, i)
         group_u2(S, 0, 2, 1)
-        group_u2(S, 1, 2, 0)
+        weight_error(V, 1, 2)
+        weight_error(V, 1, 3)
+        quantize_err(0)
         for i in range(PACK):
             gradient(0, 0, i)
-        for i in range(PACK):
-            error(1, i)
-        quantize_u2(1, 1)
-        group_err(S, 1, 352, 512)
-        group_err(V, 1, 0, 352)
-        quantize_u2(0, 2)
+        group_err(S, 1, 256, 512)
+        group_err(V, 1, 0, 256)
+        group_u2(V, 1, 2, 0)
         group_u2(S, 1, 2, 1)
         quantize_err(1)
         for i in range(PACK):
@@ -338,35 +392,58 @@ def tile_freshcyclicfilterblocklmsupdate_x1_kernel(tc, x, d, w, phase, v, mu, ou
         for i in range(2):
             gradient(0, 1, i)
             gradient(1, 1, i)
+        quantize_u2(0, 2)
         quantize_u2(1, 2)
-        group_u2(S, 0, 3, 0)
-        group_u2(S, 0, 3, 1)
-        group_u2(S, 1, 3, 0)
-        group_u2(S, 1, 3, 1)
+        for g in range(G):
+            group_u2(S, g, 3, 0)
+            group_u2(S, g, 3, 1)
         tiles = [(a, i) for a in range(A) for i in range(PACK)]
-        for n in range(len(tiles) + 3):
-            if n < len(tiles):
-                a, i = tiles[n]
-                update(a, i)
-                if i % 2 == 1:
-                    store_result(a, i - 1, i + 1)
-            if n == 3:
+        rounder = [Q, Q, Q, Q, S, Q, Q, Q, S, S, S, S, Q, S, Q]
+        turn_after = {3: 0, 5: 1, 7: 2, 8: 3, 10: 4, 12: 5, 14: 6}
+        gather_after = {4: [0, 1][:1], 5: [1], 8: [2], 10: [3], 11: [4], 13: [5], 14: [6]}
+        gradients_after = {0: 6, 3: 8, 5: 10, 9: 12, 10: 14}
+        last = len(tiles) - 1
+        for n in range(last + 1):
+            a, i = tiles[n]
+            if n == last:
+                update_rounded(a, i)
+            update(a, i)
+            if i % 2 == 1:
+                store_result(a, i - 1, i + 1)
+            if n == 9:
                 quantize_u2(0, 3)
-            if n == 5:
                 quantize_u2(1, 3)
-            if 1 <= n <= len(tiles):
-                pa, pi = tiles[n - 1]
-                round_result(V if (n - 1 < 6 or n - 1 in (9, 13, 15)) else S, pa, pi)
-                if pi % 2 == 1:
-                    turn_result(pa, pi // 2)
-            if n + 6 < len(tiles):
-                gradient(0, *tiles[n + 6])
-                gradient(1, *tiles[n + 6])
-            if 2 <= n - 1 <= len(tiles) + 1:
-                pa, pi = tiles[n - 3]
-                if pi % 2 == 1:
-                    gather_plane(S, pa, pi // 2)
-            if n >= 8 and n % 4 == 0:
-                quantize_plane(n // 4 - 2)
-        quantize_plane(A - 1)
+            if n == 11:
+                quantize_plane(0)
+            if n < last:
+                round_result(rounder[n], a, i)
+            if n in (0, 1, 9):
+                pass
+            if n in turn_after and n != 10:
+                pair = turn_after[n]
+                turn_result(*tiles[2 * pair])
+                turn_result(*tiles[2 * pair + 1])
+            if n in (1, 9):
+                m = {1: 6, 9: 12}[n]
+                for t in (m, m + 1):
+                    gradient(0, *tiles[t])
+                    gradient(1, *tiles[t])
+            if n == 10:
+                turn_result(*tiles[8])
+                turn_result(*tiles[9])
+            if n in (3, 5, 10):
+                m = {3: 8, 5: 10, 10: 14}[n]
+                for t in (m, m + 1):
+                    gradient(0, *tiles[t])
+                    gradient(1, *tiles[t])
+            for pair in gather_after.get(n, []):
+                gather_plane(S, pair // 2, pair % 2)
+        quantize_plane(1)
+        turn_result(3, 2)
+        turn_result(3, 3, natural=True)
+        quantize_plane(2)
+        gather_plane(V, 3, 1, 0, 64)
+        gather_plane(S, 3, 1, 64, 128)
+        quantize_plane(3, 256, 512)
+        quantize_plane(3, 0, 256)
         store_scales()

@@ -66,7 +66,7 @@ def tile_freshcyclicfilterblocklmsupdate_x1_kernel(tc, x, d, w, phase, v, mu, ou
 
         phase_sb = kept("phase_sb", [P, A * G, PAD], BF16)
         v_sb = kept("v_sb", [P, G, PAD], BF16)
-        mu_sb = kept("mu_sb", [P, A, PAD], BF16)
+        mu_sb = kept("mu_sb", [P, 2 * A, PAD], BF16)
         x_rows = [kept("x_rows%d" % g, [P, PACK, L], BF16) for g in range(G)]
         d_rows = [kept("d_rows%d" % g, [P, PACK, J], BF16) for g in range(G)]
         w_rows = [kept("w_rows%d" % a, [P, PACK, J], BF16) for a in range(A)]
@@ -74,19 +74,29 @@ def tile_freshcyclicfilterblocklmsupdate_x1_kernel(tc, x, d, w, phase, v, mu, ou
         def load_rows(dst, src):
             nc.sync.dma_start(out=dst[:], in_=src.rearrange("(p i) c -> p i c", i=PACK))
 
-        nc.scalar.dma_start(out=phase_sb[:, :, 0:PACK], in_=phase.rearrange("a (g p i) -> p (a g) i", g=G, i=PACK))
+        def load_w(a):
+            halves = w[a].rearrange("(b u r e) j -> u b r (e j)", u=2, r=8, e=2)
+            for u in range(2):
+                nc.sync.dma_start(out=w_rows[a][:, 2 * u : 2 * u + 2, :].rearrange("q e j -> q (e j)"), in_=halves[u])
+
+        phase_rows = phase.rearrange("a (g p i) -> p g a i", g=G, i=PACK)
+        nc.scalar.dma_start(out=phase_sb[:, 0:A, 0:PACK], in_=phase_rows[:, 0])
         x_first = x[0:512, :].rearrange("(p i) c -> p i c", i=PACK)
         nc.sync.dma_start(out=x_rows[0][:, 0:2, :], in_=x_first[:, 0:2, :])
         nc.sync.dma_start(out=x_rows[0][:, 2:4, :], in_=x_first[:, 2:4, :])
-        load_rows(w_rows[0], w[0])
-        load_rows(w_rows[1], w[1])
+        load_w(0)
+        load_w(1)
+        nc.sync.dma_start(out=phase_sb[:, A : 2 * A, 0:PACK], in_=phase_rows[:, 1])
         load_rows(x_rows[1], x[512:1024, :])
-        load_rows(w_rows[2], w[2])
+        load_w(2)
+        load_w(3)
         nc.sync.dma_start(out=v_sb[:, :, 0:PACK], in_=v.rearrange("(g p i) -> p g i", g=G, i=PACK))
-        load_rows(w_rows[3], w[3])
         load_rows(d_rows[0], d[0:512, :])
         load_rows(d_rows[1], d[512:1024, :])
-        nc.sync.dma_start(out=mu_sb[:, :, 0:PACK], in_=mu.rearrange("a (q i) -> q a i", i=PACK))
+        mu_halves = mu.rearrange("a (b u r e) -> a u b r e", u=2, r=8, e=2)
+        for a in range(A):
+            for u in range(2):
+                nc.sync.dma_start(out=mu_sb[:, 2 * a + u, 0:2], in_=mu_halves[a, u])
 
         ident = kept("ident", [P, P], F32)
         make_identity(nc, ident[:])
@@ -113,12 +123,16 @@ def tile_freshcyclicfilterblocklmsupdate_x1_kernel(tc, x, d, w, phase, v, mu, ou
         plane_codes = kept("plane_codes", [P, A * L], U32)
         plane_scales = kept("plane_scales", [P, A * L], U8)
 
-        def cosine():
+        def fold_phase(g):
+            rows = slice(A * g, A * (g + 1))
             nc.vector.scalar_tensor_tensor(
-                out=neg_abs[:], in0=phase_sb[:, :, 0:PACK], scalar=-1.0, in1=phase_sb[:, :, 0:PACK],
+                out=neg_abs[:, rows, :], in0=phase_sb[:, rows, 0:PACK], scalar=-1.0, in1=phase_sb[:, rows, 0:PACK],
                 op0=ALU.mult, op1=ALU.min,
             )
-            nc.scalar.activation(out=cos_sb[:], in_=neg_abs[:], func=ACT.Sin, bias=math.pi / 2)
+
+        def cosine(g):
+            rows = slice(A * g, A * (g + 1))
+            nc.scalar.activation(out=cos_sb[:, rows, :], in_=neg_abs[:, rows, :], func=ACT.Sin, bias=math.pi / 2)
 
         def widen_v():
             nc.vector.tensor_copy(out=v_f32[:], in_=v_sb[:, :, 0:PACK])
@@ -127,8 +141,9 @@ def tile_freshcyclicfilterblocklmsupdate_x1_kernel(tc, x, d, w, phase, v, mu, ou
             u_rows[g, a] = kept("u_rows%d%d" % (g, a), [P, PACK, L], BF16)
             for i in range(PACK):
                 nc.vector.tensor_scalar(
-                    out=u_rows[g, a][:, i, :], in0=x_rows[g][:, i, :],
-                    scalar1=cos_sb[:, a * G + g, i : i + 1], scalar2=None, op0=ALU.mult,
+                    out=u_rows[g, a][:, i, :].rearrange("p (u b c) -> p u b c", u=2, c=16),
+                    in0=x_rows[g][:, i, :].rearrange("p (b u c) -> p u b c", u=2, c=16),
+                    scalar1=cos_sb[:, A * g + a, i : i + 1], scalar2=None, op0=ALU.mult,
                 )
 
         def turn_u(g, a, half):
@@ -138,7 +153,7 @@ def tile_freshcyclicfilterblocklmsupdate_x1_kernel(tc, x, d, w, phase, v, mu, ou
                 for n in range(4):
                     i, u = 2 * half + n // 2, n % 2
                     nc.tensor.transpose(
-                        u1_banks[g, a, half][:, n, :], words[:, 256 * i + u : 256 * (i + 1) : 2], ident[:]
+                        u1_banks[g, a, half][:, n, :], words[:, 256 * i + P * u : 256 * i + P * (u + 1)], ident[:]
                     )
 
         def gather_u1(engine, g, a, half):
@@ -210,7 +225,7 @@ def tile_freshcyclicfilterblocklmsupdate_x1_kernel(tc, x, d, w, phase, v, mu, ou
             copy_on(
                 engine,
                 u2_grouped[g, a][:, cols, :].rearrange("p (e c r) i -> p c i r e", e=2, r=2),
-                u_rows[g, a][:].rearrange("p i (c r u e) -> p c i r u e", r=2, u=2, e=2)[:, :, :, :, u, :],
+                u_rows[g, a][:, :, cols].rearrange("p i (c r e) -> p c i r e", r=2, e=2),
             )
 
         def quantize_u2(g, a):
@@ -223,13 +238,15 @@ def tile_freshcyclicfilterblocklmsupdate_x1_kernel(tc, x, d, w, phase, v, mu, ou
 
         def update(a, i):
             nc.vector.scalar_tensor_tensor(
-                out=result[a][:, i, :], in0=grad[a, i][:], scalar=mu_sb[:, a, i : i + 1], in1=w_rows[a][:, i, :],
+                out=result[a][:, i, :], in0=grad[a, i][:], scalar=mu_sb[:, 2 * a + i // 2, i % 2 : i % 2 + 1], in1=w_rows[a][:, i, :],
                 op0=ALU.mult, op1=ALU.add,
             )
 
         def store_result(a, first, last):
+            halves = out_0[a].rearrange("(b u r e) j -> u b r (e j)", u=2, r=8, e=2)
+            cols = slice(J * (first % 2), J * (first % 2 + last - first))
             nc.sync.dma_start(
-                out=out_0[a].rearrange("(q i) j -> q i j", i=PACK)[:, first:last, :], in_=result[a][:, first:last, :]
+                out=halves[first // 2][:, :, cols], in_=result[a][:, first:last, :].rearrange("q e j -> q (e j)")
             )
 
         def round_result(engine, a, i):
@@ -244,7 +261,7 @@ def tile_freshcyclicfilterblocklmsupdate_x1_kernel(tc, x, d, w, phase, v, mu, ou
 
         def update_rounded(a, i):
             nc.vector.scalar_tensor_tensor(
-                out=result_bf[a][:, i, :], in0=grad[a, i][:], scalar=mu_sb[:, a, i : i + 1], in1=w_rows[a][:, i, :],
+                out=result_bf[a][:, i, :], in0=grad[a, i][:], scalar=mu_sb[:, 2 * a + i // 2, i % 2 : i % 2 + 1], in1=w_rows[a][:, i, :],
                 op0=ALU.mult, op1=ALU.add,
             )
 
@@ -257,14 +274,14 @@ def tile_freshcyclicfilterblocklmsupdate_x1_kernel(tc, x, d, w, phase, v, mu, ou
                 src = words[:, u:256:2] if natural else words[:, u * P : (u + 1) * P]
                 nc.tensor.transpose(plane_banks[a, half][:, 2 * (i % 2) + u, :], src, ident[:])
 
-        def gather_plane(engine, a, half, first=0, last=P):
+        def gather_plane(engine, a, half, first=0, last=16):
             if a not in plane_grouped:
                 plane_grouped[a] = staged("plane_grouped", "plane_grouped%d" % a, [P, L, PACK], BF16)
             words = plane_grouped[a][:].rearrange("p m k -> p (m k)").bitcast(F32)
             copy_on(
                 engine,
-                words.rearrange("p (q i u) -> p q i u", i=PACK, u=2)[:, first:last, 2 * half : 2 * half + 2, :],
-                plane_banks[a, half][:].rearrange("p (i u) q -> p q i u", u=2)[:, first:last],
+                words.rearrange("p (b h r e u) -> p h b r e u", h=2, r=8, e=2, u=2)[:, half, first:last],
+                plane_banks[a, half][:].rearrange("p (e u) (b r) -> p b r e u", u=2, r=8)[:, first:last],
             )
 
         def quantize_plane(a, first=0, last=L):
@@ -301,7 +318,8 @@ def tile_freshcyclicfilterblocklmsupdate_x1_kernel(tc, x, d, w, phase, v, mu, ou
                 quantize_u1(*steps[k], half)
                 estimate(*steps[k], half)
 
-        cosine()
+        fold_phase(0)
+        cosine(0)
         modulate_and_turn(0)
         group_u2(S, 0, 0, 0)
         modulate_and_turn(1)
@@ -312,9 +330,11 @@ def tile_freshcyclicfilterblocklmsupdate_x1_kernel(tc, x, d, w, phase, v, mu, ou
         turn_u(*steps[2], 1)
         modulate(*steps[3])
         group_u2(S, 0, 0, 1)
+        fold_phase(1)
         quantize_w(0)
         group_w(V, 1, 0, 512)
         stage_one(0)
+        cosine(1)
         gather(1)
         turn_u(*steps[3], 0)
         turn_u(*steps[3], 1)
@@ -398,52 +418,43 @@ def tile_freshcyclicfilterblocklmsupdate_x1_kernel(tc, x, d, w, phase, v, mu, ou
             group_u2(S, g, 3, 0)
             group_u2(S, g, 3, 1)
         tiles = [(a, i) for a in range(A) for i in range(PACK)]
-        rounder = [Q, Q, Q, Q, S, Q, Q, Q, S, S, S, S, Q, S, Q]
-        turn_after = {3: 0, 5: 1, 7: 2, 8: 3, 10: 4, 12: 5, 14: 6}
-        gather_after = {4: [0, 1][:1], 5: [1], 8: [2], 10: [3], 11: [4], 13: [5], 14: [6]}
-        gradients_after = {0: 6, 3: 8, 5: 10, 9: 12, 10: 14}
+        rounder = [Q, Q, Q, Q, S, Q, Q, Q, S, S, S, Q, Q, S, S]
+        turn_after = {2: 0, 4: 1, 7: 2, 9: 3, 10: 4, 12: 5, 14: 6}
+        gather_after = {4: 0, 5: 1, 8: 2, 9: 3, 11: 4, 14: 5}
+        gradients_after = {1: (6, 7), 3: (8, 9), 5: (10, 11), 10: (12, 13), 11: (14, 15)}
         last = len(tiles) - 1
-        for n in range(last + 1):
+        for n in range(last):
             a, i = tiles[n]
-            if n == last:
-                update_rounded(a, i)
             update(a, i)
             if i % 2 == 1:
                 store_result(a, i - 1, i + 1)
-            if n == 9:
+            if n == 10:
                 quantize_u2(0, 3)
                 quantize_u2(1, 3)
-            if n == 11:
                 quantize_plane(0)
             if n < last:
                 round_result(rounder[n], a, i)
-            if n in (0, 1, 9):
-                pass
-            if n in turn_after and n != 10:
+            if n in gradients_after:
+                for t in gradients_after[n]:
+                    gradient(0, *tiles[t])
+                    gradient(1, *tiles[t])
+            if n in turn_after:
                 pair = turn_after[n]
                 turn_result(*tiles[2 * pair])
                 turn_result(*tiles[2 * pair + 1])
-            if n in (1, 9):
-                m = {1: 6, 9: 12}[n]
-                for t in (m, m + 1):
-                    gradient(0, *tiles[t])
-                    gradient(1, *tiles[t])
-            if n == 10:
-                turn_result(*tiles[8])
-                turn_result(*tiles[9])
-            if n in (3, 5, 10):
-                m = {3: 8, 5: 10, 10: 14}[n]
-                for t in (m, m + 1):
-                    gradient(0, *tiles[t])
-                    gradient(1, *tiles[t])
-            for pair in gather_after.get(n, []):
-                gather_plane(S, pair // 2, pair % 2)
+            if n in gather_after:
+                gather_plane(S, gather_after[n] // 2, gather_after[n] % 2)
+        store_result(3, 2, 3)
+        update_rounded(3, 3)
         quantize_plane(1)
         turn_result(3, 2)
         turn_result(3, 3, natural=True)
+        gather_plane(S, 3, 0)
+        update(3, 3)
+        store_result(3, 3, 4)
         quantize_plane(2)
-        gather_plane(V, 3, 1, 0, 64)
-        gather_plane(S, 3, 1, 64, 128)
-        quantize_plane(3, 256, 512)
+        gather_plane(S, 3, 1, 0, 8)
+        gather_plane(S, 3, 1, 8, 16)
         quantize_plane(3, 0, 256)
+        quantize_plane(3, 256, 512)
         store_scales()

@@ -66,7 +66,7 @@ def tile_freshcyclicfilterblocklmsupdate_x1_kernel(tc, x, d, w, phase, v, mu, ou
 
         phase_sb = kept("phase_sb", [P, A * G, PAD], BF16)
         v_sb = kept("v_sb", [P, G, PAD], BF16)
-        mu_sb = kept("mu_sb", [P, 2 * A, PAD], BF16)
+        mu_sb = kept("mu_sb", [P, A, PAD], BF16)
         x_rows = [kept("x_rows%d" % g, [P, PACK, L], BF16) for g in range(G)]
         d_rows = [kept("d_rows%d" % g, [P, PACK, J], BF16) for g in range(G)]
         w_rows = [kept("w_rows%d" % a, [P, PACK, J], BF16) for a in range(A)]
@@ -74,29 +74,21 @@ def tile_freshcyclicfilterblocklmsupdate_x1_kernel(tc, x, d, w, phase, v, mu, ou
         def load_rows(dst, src):
             nc.sync.dma_start(out=dst[:], in_=src.rearrange("(p i) c -> p i c", i=PACK))
 
-        def load_w(a):
-            halves = w[a].rearrange("(b u r e) j -> u b r (e j)", u=2, r=8, e=2)
-            for u in range(2):
-                nc.sync.dma_start(out=w_rows[a][:, 2 * u : 2 * u + 2, :].rearrange("q e j -> q (e j)"), in_=halves[u])
-
         phase_rows = phase.rearrange("a (g p i) -> p g a i", g=G, i=PACK)
         nc.scalar.dma_start(out=phase_sb[:, 0:A, 0:PACK], in_=phase_rows[:, 0])
         x_first = x[0:512, :].rearrange("(p i) c -> p i c", i=PACK)
         nc.sync.dma_start(out=x_rows[0][:, 0:2, :], in_=x_first[:, 0:2, :])
         nc.sync.dma_start(out=x_rows[0][:, 2:4, :], in_=x_first[:, 2:4, :])
-        load_w(0)
-        load_w(1)
+        load_rows(w_rows[0], w[0])
+        load_rows(w_rows[1], w[1])
         nc.sync.dma_start(out=phase_sb[:, A : 2 * A, 0:PACK], in_=phase_rows[:, 1])
         load_rows(x_rows[1], x[512:1024, :])
-        load_w(2)
-        load_w(3)
+        load_rows(w_rows[2], w[2])
         nc.sync.dma_start(out=v_sb[:, :, 0:PACK], in_=v.rearrange("(g p i) -> p g i", g=G, i=PACK))
+        load_rows(w_rows[3], w[3])
         load_rows(d_rows[0], d[0:512, :])
         load_rows(d_rows[1], d[512:1024, :])
-        mu_halves = mu.rearrange("a (b u r e) -> a u b r e", u=2, r=8, e=2)
-        for a in range(A):
-            for u in range(2):
-                nc.sync.dma_start(out=mu_sb[:, 2 * a + u, 0:2], in_=mu_halves[a, u])
+        nc.sync.dma_start(out=mu_sb[:, :, 0:PACK], in_=mu.rearrange("a (q i) -> q a i", i=PACK))
 
         ident = kept("ident", [P, P], F32)
         make_identity(nc, ident[:])
@@ -108,6 +100,7 @@ def tile_freshcyclicfilterblocklmsupdate_x1_kernel(tc, x, d, w, phase, v, mu, ou
         neg_abs = kept("neg_abs", [P, A * G, PACK], F32)
         cos_sb = kept("cos_sb", [P, A * G, PACK], F32)
         v_f32 = kept("v_f32", [P, G, PACK], F32)
+        x_perm = [kept("x_perm%d" % g, [P, PACK, L], BF16) for g in range(G)]
         u_rows = {}
         u1_banks, u1_grouped, u1_q = {}, {}, {}
         w_grouped, w_q = {}, {}
@@ -137,12 +130,16 @@ def tile_freshcyclicfilterblocklmsupdate_x1_kernel(tc, x, d, w, phase, v, mu, ou
         def widen_v():
             nc.vector.tensor_copy(out=v_f32[:], in_=v_sb[:, :, 0:PACK])
 
+        def permute_x(engine, g, first, last):
+            src = x_rows[g][:, first:last, :].rearrange("p i l -> p (i l)").bitcast(F32)
+            dst = x_perm[g][:, first:last, :].rearrange("p i l -> p (i l)").bitcast(F32)
+            copy_on(engine, dst.rearrange("p (i u q) -> p i u q", u=2, q=P), src.rearrange("p (i q u) -> p i u q", u=2, q=P))
+
         def modulate(g, a):
             u_rows[g, a] = kept("u_rows%d%d" % (g, a), [P, PACK, L], BF16)
             for i in range(PACK):
                 nc.vector.tensor_scalar(
-                    out=u_rows[g, a][:, i, :].rearrange("p (u b c) -> p u b c", u=2, c=16),
-                    in0=x_rows[g][:, i, :].rearrange("p (b u c) -> p u b c", u=2, c=16),
+                    out=u_rows[g, a][:, i, :], in0=(x_perm if g in PERM else x_rows)[g][:, i, :],
                     scalar1=cos_sb[:, A * g + a, i : i + 1], scalar2=None, op0=ALU.mult,
                 )
 
@@ -153,7 +150,7 @@ def tile_freshcyclicfilterblocklmsupdate_x1_kernel(tc, x, d, w, phase, v, mu, ou
                 for n in range(4):
                     i, u = 2 * half + n // 2, n % 2
                     nc.tensor.transpose(
-                        u1_banks[g, a, half][:, n, :], words[:, 256 * i + P * u : 256 * i + P * (u + 1)], ident[:]
+                        u1_banks[g, a, half][:, n, :], (words[:, 256 * i + P * u : 256 * i + P * (u + 1)] if g in PERM else words[:, 256 * i + u : 256 * (i + 1) : 2]), ident[:]
                     )
 
         def gather_u1(engine, g, a, half):
@@ -225,7 +222,7 @@ def tile_freshcyclicfilterblocklmsupdate_x1_kernel(tc, x, d, w, phase, v, mu, ou
             copy_on(
                 engine,
                 u2_grouped[g, a][:, cols, :].rearrange("p (e c r) i -> p c i r e", e=2, r=2),
-                u_rows[g, a][:, :, cols].rearrange("p i (c r e) -> p c i r e", r=2, e=2),
+                u_rows[g, a][:, :, cols].rearrange("p i (c r e) -> p c i r e", r=2, e=2) if g in PERM else u_rows[g, a][:].rearrange("p i (c r u e) -> p c i r u e", r=2, u=2, e=2)[:, :, :, :, u, :],
             )
 
         def quantize_u2(g, a):
@@ -238,15 +235,13 @@ def tile_freshcyclicfilterblocklmsupdate_x1_kernel(tc, x, d, w, phase, v, mu, ou
 
         def update(a, i):
             nc.vector.scalar_tensor_tensor(
-                out=result[a][:, i, :], in0=grad[a, i][:], scalar=mu_sb[:, 2 * a + i // 2, i % 2 : i % 2 + 1], in1=w_rows[a][:, i, :],
+                out=result[a][:, i, :], in0=grad[a, i][:], scalar=mu_sb[:, a, i : i + 1], in1=w_rows[a][:, i, :],
                 op0=ALU.mult, op1=ALU.add,
             )
 
         def store_result(a, first, last):
-            halves = out_0[a].rearrange("(b u r e) j -> u b r (e j)", u=2, r=8, e=2)
-            cols = slice(J * (first % 2), J * (first % 2 + last - first))
             nc.sync.dma_start(
-                out=halves[first // 2][:, :, cols], in_=result[a][:, first:last, :].rearrange("q e j -> q (e j)")
+                out=out_0[a].rearrange("(q i) j -> q i j", i=PACK)[:, first:last, :], in_=result[a][:, first:last, :]
             )
 
         def round_result(engine, a, i):
@@ -261,7 +256,7 @@ def tile_freshcyclicfilterblocklmsupdate_x1_kernel(tc, x, d, w, phase, v, mu, ou
 
         def update_rounded(a, i):
             nc.vector.scalar_tensor_tensor(
-                out=result_bf[a][:, i, :], in0=grad[a, i][:], scalar=mu_sb[:, 2 * a + i // 2, i % 2 : i % 2 + 1], in1=w_rows[a][:, i, :],
+                out=result_bf[a][:, i, :], in0=grad[a, i][:], scalar=mu_sb[:, a, i : i + 1], in1=w_rows[a][:, i, :],
                 op0=ALU.mult, op1=ALU.add,
             )
 
@@ -274,14 +269,14 @@ def tile_freshcyclicfilterblocklmsupdate_x1_kernel(tc, x, d, w, phase, v, mu, ou
                 src = words[:, u:256:2] if natural else words[:, u * P : (u + 1) * P]
                 nc.tensor.transpose(plane_banks[a, half][:, 2 * (i % 2) + u, :], src, ident[:])
 
-        def gather_plane(engine, a, half, first=0, last=16):
+        def gather_plane(engine, a, half, first=0, last=P):
             if a not in plane_grouped:
                 plane_grouped[a] = staged("plane_grouped", "plane_grouped%d" % a, [P, L, PACK], BF16)
             words = plane_grouped[a][:].rearrange("p m k -> p (m k)").bitcast(F32)
             copy_on(
                 engine,
-                words.rearrange("p (b h r e u) -> p h b r e u", h=2, r=8, e=2, u=2)[:, half, first:last],
-                plane_banks[a, half][:].rearrange("p (e u) (b r) -> p b r e u", u=2, r=8)[:, first:last],
+                words.rearrange("p (q i u) -> p q i u", i=PACK, u=2)[:, first:last, 2 * half : 2 * half + 2, :],
+                plane_banks[a, half][:].rearrange("p (i u) q -> p q i u", u=2)[:, first:last],
             )
 
         def quantize_plane(a, first=0, last=L):
@@ -301,6 +296,7 @@ def tile_freshcyclicfilterblocklmsupdate_x1_kernel(tc, x, d, w, phase, v, mu, ou
                     in_=plane_scales[32 * quad : 32 * quad + 4, :].bitcast(I32),
                 )
 
+        PERM = (1,)
         V, S, Q = "vector", "scalar", "gpsimd"
         steps = [(g, a) for g in range(G) for a in range(A)]
 
@@ -331,6 +327,7 @@ def tile_freshcyclicfilterblocklmsupdate_x1_kernel(tc, x, d, w, phase, v, mu, ou
         modulate(*steps[3])
         group_u2(S, 0, 0, 1)
         fold_phase(1)
+        permute_x(V, 1, 0, 4)
         quantize_w(0)
         group_w(V, 1, 0, 512)
         stage_one(0)
@@ -381,16 +378,15 @@ def tile_freshcyclicfilterblocklmsupdate_x1_kernel(tc, x, d, w, phase, v, mu, ou
         estimate(*steps[4], 1)
         gather(6)
         stage_one(5)
+        weight_error(S, 0, 2)
+        weight_error(S, 0, 3)
         gather(7)
         quantize_u2(1, 0)
         stage_one(6)
-        weight_error(S, 0, 2)
-        weight_error(S, 0, 3)
         group_u2(V, 1, 1, 1)
         stage_one(7)
+        group_err(S, 0, 0, 512)
         group_u2(S, 0, 2, 0)
-        group_err(S, 0, 96, 512)
-        group_err(V, 0, 0, 96)
         quantize_u2(1, 1)
         for i in range(PACK):
             subtract_estimate(1, i)
@@ -400,18 +396,18 @@ def tile_freshcyclicfilterblocklmsupdate_x1_kernel(tc, x, d, w, phase, v, mu, ou
         weight_error(V, 1, 2)
         weight_error(V, 1, 3)
         quantize_err(0)
-        for i in range(PACK):
-            gradient(0, 0, i)
-        group_err(S, 1, 256, 512)
-        group_err(V, 1, 0, 256)
+        for n in range(4):
+            gradient(0, n // PACK, n % PACK)
+        group_err(S, 1, 288, 512)
+        group_err(V, 1, 0, 288)
         group_u2(V, 1, 2, 0)
         group_u2(S, 1, 2, 1)
         quantize_err(1)
-        for i in range(PACK):
-            gradient(1, 0, i)
-        for i in range(2):
-            gradient(0, 1, i)
-            gradient(1, 1, i)
+        for n in range(4):
+            gradient(1, n // PACK, n % PACK)
+        for n in range(4, 6):
+            gradient(0, n // PACK, n % PACK)
+            gradient(1, n // PACK, n % PACK)
         quantize_u2(0, 2)
         quantize_u2(1, 2)
         for g in range(G):
@@ -421,7 +417,7 @@ def tile_freshcyclicfilterblocklmsupdate_x1_kernel(tc, x, d, w, phase, v, mu, ou
         rounder = [Q, Q, Q, Q, S, Q, Q, Q, S, S, S, Q, Q, S, S]
         turn_after = {2: 0, 4: 1, 7: 2, 9: 3, 10: 4, 12: 5, 14: 6}
         gather_after = {4: 0, 5: 1, 8: 2, 9: 3, 11: 4, 14: 5}
-        gradients_after = {1: (6, 7), 3: (8, 9), 5: (10, 11), 10: (12, 13), 11: (14, 15)}
+        gradients_after = {1: (6, 7), 3: (8, 9), 5: (10, 11), 10: (12, 13, 14), 11: (15,)}
         last = len(tiles) - 1
         for n in range(last):
             a, i = tiles[n]
@@ -453,8 +449,8 @@ def tile_freshcyclicfilterblocklmsupdate_x1_kernel(tc, x, d, w, phase, v, mu, ou
         update(3, 3)
         store_result(3, 3, 4)
         quantize_plane(2)
-        gather_plane(S, 3, 1, 0, 8)
-        gather_plane(S, 3, 1, 8, 16)
+        gather_plane(S, 3, 1, 0, 64)
+        gather_plane(S, 3, 1, 64, 128)
         quantize_plane(3, 0, 256)
         quantize_plane(3, 256, 512)
         store_scales()

@@ -18,8 +18,18 @@ ACT = mybir.ActivationFunctionType
 
 P = 128
 PACK = 4
-G = T // (P * PACK)
-PAD = 16
+K_PASS = P * PACK
+G = T // K_PASS
+HALF = K_PASS // 2
+PITCH = 16
+RUN = 4
+
+EST_BANK, GRAD_BANKS, PLANE_BANK, LAST_PLANE_BANK = 4, 6, 6, 4
+
+VECTOR, SCALAR, GPSIMD = "vector", "scalar", "gpsimd"
+
+W_SPLIT = (J, J, 192, 0)
+ERR_SPLIT = (96, 256)
 
 
 def tile_freshcyclicfilterblocklmsupdate_x1_kernel(tc, x, d, w, phase, v, mu, out_0, out_1, out_2):
@@ -40,147 +50,28 @@ def tile_freshcyclicfilterblocklmsupdate_x1_kernel(tc, x, d, w, phase, v, mu, ou
             return psum.tile(shape, F32, name=name, tag="bank%d" % number)
 
         def copy_on(engine, out, in_):
-            if engine == "vector":
+            if engine == VECTOR:
                 nc.vector.tensor_copy(out=out, in_=in_)
             else:
                 nc.scalar.copy(out=out, in_=in_)
 
-        def quantize(name, grouped, tag=None):
-            if tag is None:
-                codes = kept(name + "_codes", [P, 512], U32)
-                scales = kept(name + "_scales", [P, 512], U8)
-            else:
-                codes = staged(tag + "_codes", name + "_codes", [P, 512], U32)
-                scales = staged(tag + "_scales", name + "_scales", [P, 512], U8)
-            nc.vector.quantize_mx(
-                out=codes[:].bitcast(FP8X4), scales=scales[:], in_=grouped[:].rearrange("p c i -> p (c i)")
-            )
+        def quantize_columns(codes, scales, grouped):
+            nc.vector.quantize_mx(out=codes.bitcast(FP8X4), scales=scales, in_=grouped.rearrange("p c i -> p (c i)"))
+
+        def quantize_kept(name, grouped):
+            codes = kept(name + "_codes", [P, K_PASS], U32)
+            scales = kept(name + "_scales", [P, K_PASS], U8)
+            quantize_columns(codes[:], scales[:], grouped[:])
             return codes, scales
 
-        def interleave(engine, grouped, rows, first, last):
-            copy_on(
-                engine,
-                grouped[:, first:last, :].rearrange("p (c r) i -> p c i r", r=4),
-                rows[:, :, first:last].rearrange("p i (c r) -> p c i r", r=4),
-            )
-
-        phase_sb = kept("phase_sb", [P, A * G, PAD], BF16)
-        v_sb = kept("v_sb", [P, G, PAD], BF16)
-        mu_sb = kept("mu_sb", [P, A, PAD], BF16)
-        x_rows = [kept("x_rows%d" % g, [P, PACK, L], BF16) for g in range(G)]
-        d_rows = [kept("d_rows%d" % g, [P, PACK, J], BF16) for g in range(G)]
-        w_rows = [kept("w_rows%d" % a, [P, PACK, J], BF16) for a in range(A)]
-
-        def load_rows(dst, src):
-            nc.sync.dma_start(out=dst[:], in_=src.rearrange("(p i) c -> p i c", i=PACK))
-
-        phase_rows = phase.rearrange("a (g p i) -> p g a i", g=G, i=PACK)
-        nc.scalar.dma_start(out=phase_sb[:, 0:A, 0:PACK], in_=phase_rows[:, 0])
-        x_first = x[0:512, :].rearrange("(p i) c -> p i c", i=PACK)
-        nc.sync.dma_start(out=x_rows[0][:, 0:2, :], in_=x_first[:, 0:2, :])
-        nc.sync.dma_start(out=x_rows[0][:, 2:4, :], in_=x_first[:, 2:4, :])
-        load_rows(w_rows[0], w[0])
-        load_rows(w_rows[1], w[1])
-        nc.sync.dma_start(out=phase_sb[:, A : 2 * A, 0:PACK], in_=phase_rows[:, 1])
-        load_rows(x_rows[1], x[512:1024, :])
-        load_rows(w_rows[2], w[2])
-        nc.sync.dma_start(out=v_sb[:, :, 0:PACK], in_=v.rearrange("(g p i) -> p g i", g=G, i=PACK))
-        load_rows(w_rows[3], w[3])
-        load_rows(d_rows[0], d[0:512, :])
-        load_rows(d_rows[1], d[512:1024, :])
-        nc.sync.dma_start(out=mu_sb[:, :, 0:PACK], in_=mu.rearrange("a (q i) -> q a i", i=PACK))
-
-        ident = kept("ident", [P, P], F32)
-        make_identity(nc, ident[:])
-        warm_in = kept("warm_in", [P, 1], F32)
-        warm_out = kept("warm_out", [P, 1], F32)
-        nc.vector.memset(warm_in[:], 0.0)
-        nc.scalar.activation(out=warm_out[:], in_=warm_in[:], func=ACT.Sin)
-
-        neg_abs = kept("neg_abs", [P, A * G, PACK], F32)
-        cos_sb = kept("cos_sb", [P, A * G, PACK], F32)
-        v_f32 = kept("v_f32", [P, G, PACK], F32)
-        x_perm = [kept("x_perm%d" % g, [P, PACK, L], BF16) for g in range(G)]
-        u_rows = {}
-        u1_banks, u1_grouped, u1_q = {}, {}, {}
-        w_grouped, w_q = {}, {}
-        est = {}
-        diff = {}
-        err_rows = [kept("err_rows%d" % g, [P, PACK, J], BF16) for g in range(G)]
-        err_grouped = [kept("err_grouped%d" % g, [P, J, PACK], BF16) for g in range(G)]
-        err_q = {}
-        u2_grouped, u2_q = {}, {}
-        grad = {}
-        result = [kept("result%d" % a, [P, PACK, J], F32) for a in range(A)]
-        result_bf, plane_banks, plane_grouped = {}, {}, {}
-        plane_codes = kept("plane_codes", [P, A * L], U32)
-        plane_scales = kept("plane_scales", [P, A * L], U8)
-
-        def fold_phase(g):
-            rows = slice(A * g, A * (g + 1))
-            nc.vector.scalar_tensor_tensor(
-                out=neg_abs[:, rows, :], in0=phase_sb[:, rows, 0:PACK], scalar=-1.0, in1=phase_sb[:, rows, 0:PACK],
-                op0=ALU.mult, op1=ALU.min,
-            )
-
-        def cosine(g):
-            rows = slice(A * g, A * (g + 1))
-            nc.scalar.activation(out=cos_sb[:, rows, :], in_=neg_abs[:, rows, :], func=ACT.Sin, bias=math.pi / 2)
-
-        def widen_v():
-            nc.vector.tensor_copy(out=v_f32[:], in_=v_sb[:, :, 0:PACK])
-
-        def permute_x(engine, g, first, last):
-            src = x_rows[g][:, first:last, :].rearrange("p i l -> p (i l)").bitcast(F32)
-            dst = x_perm[g][:, first:last, :].rearrange("p i l -> p (i l)").bitcast(F32)
-            copy_on(engine, dst.rearrange("p (i u q) -> p i u q", u=2, q=P), src.rearrange("p (i q u) -> p i u q", u=2, q=P))
-
-        def modulate(g, a):
-            u_rows[g, a] = kept("u_rows%d%d" % (g, a), [P, PACK, L], BF16)
-            for i in range(PACK):
-                nc.vector.tensor_scalar(
-                    out=u_rows[g, a][:, i, :], in0=(x_perm if g in PERM else x_rows)[g][:, i, :],
-                    scalar1=cos_sb[:, A * g + a, i : i + 1], scalar2=None, op0=ALU.mult,
-                )
-
-        def turn_u(g, a, half):
-            if True:
-                u1_banks[g, a, half] = bank(2 * (a % 2) + half, "u1_bank%d%d%d" % (g, a, half), [P, 4, P])
-                words = u_rows[g, a][:].rearrange("p i l -> p (i l)").bitcast(F32)
-                for n in range(4):
-                    i, u = 2 * half + n // 2, n % 2
-                    nc.tensor.transpose(
-                        u1_banks[g, a, half][:, n, :], (words[:, 256 * i + P * u : 256 * i + P * (u + 1)] if g in PERM else words[:, 256 * i + u : 256 * (i + 1) : 2]), ident[:]
+        def group_rows(grouped, rows, split):
+            for engine, first, last in ((SCALAR, split, K_PASS), (VECTOR, 0, split)):
+                if first < last:
+                    copy_on(
+                        engine,
+                        grouped[:, first:last, :].rearrange("p (c n) i -> p c i n", n=RUN),
+                        rows[:, :, first:last].rearrange("p i (c n) -> p c i n", n=RUN),
                     )
-
-        def gather_u1(engine, g, a, half):
-            if (g, a) not in u1_grouped:
-                u1_grouped[g, a] = staged("u1_grouped", "u1_grouped%d%d" % (g, a), [P, 512, PACK], BF16)
-            words = u1_grouped[g, a][:, 256 * half : 256 * (half + 1), :].rearrange("q c k -> q (c k)").bitcast(F32)
-            copy_on(
-                engine,
-                words.rearrange("q (i p u) -> q i p u", i=2, u=2),
-                u1_banks[g, a, half][:].rearrange("q (i u) p -> q i p u", u=2),
-            )
-
-        def quantize_u1(g, a, half):
-            if half == 0:
-                codes = staged("u1_codes", "u1_codes%d%d" % (g, a), [P, 512], U32)
-                scales = staged("u1_scales", "u1_scales%d%d" % (g, a), [P, 512], U8)
-                u1_q[g, a] = codes, scales
-            cols = slice(256 * half, 256 * (half + 1))
-            nc.vector.quantize_mx(
-                out=u1_q[g, a][0][:, cols].bitcast(FP8X4), scales=u1_q[g, a][1][:, cols],
-                in_=u1_grouped[g, a][:, cols, :].rearrange("p c i -> p (c i)"),
-            )
-
-        def group_w(engine, a, first, last):
-            if a not in w_grouped:
-                w_grouped[a] = staged("plane_grouped", "w_grouped%d" % a, [P, J, PACK], BF16)
-            interleave(engine, w_grouped[a], w_rows[a], first, last)
-
-        def quantize_w(a):
-            w_q[a] = quantize("w_%d" % a, w_grouped[a])
 
         def mx_pass(acc, stationary, i, moving, start, stop):
             cols = slice(i * P, (i + 1) * P)
@@ -189,268 +80,329 @@ def tile_freshcyclicfilterblocklmsupdate_x1_kernel(tc, x, d, w, phase, v, mu, ou
                 rhs=moving[0][:].bitcast(FP8X4), rhs_scale=moving[1][:], start=start, stop=stop,
             )
 
-        def estimate(g, a, half):
-            for i in range(2 * half, 2 * half + 2):
-                if a == 0:
-                    est[g, i] = bank(4 + i, "est%d%d" % (g, i), [P, J])
-                mx_pass(est[g, i], u1_q[g, a], i, w_q[a], a == 0, a == A - 1)
+        phase_sb = kept("phase_sb", [P, G * A, PITCH], BF16)
+        v_sb = kept("v_sb", [P, G, PITCH], BF16)
+        mu_sb = kept("mu_sb", [P, A, PITCH], BF16)
+        x_rows = [kept("x_rows%d" % g, [P, PACK, L], BF16) for g in range(G)]
+        d_rows = [kept("d_rows%d" % g, [P, PACK, J], BF16) for g in range(G)]
+        w_rows = [kept("w_rows%d" % a, [P, PACK, J], BF16) for a in range(A)]
 
-        def subtract_estimate(g, i):
-            if i == 0:
-                diff[g] = keep.tile([P, PACK, J], F32, name="diff%d" % g, tag="diff", align_bytes=64)
-            nc.vector.tensor_tensor(out=diff[g][:, i, :], in0=d_rows[g][:, i, :], in1=est[g, i][:], op=ALU.subtract)
+        def load_rows(dst, src, first=0, last=PACK):
+            rows = src.rearrange("(p i) c -> p i c", i=PACK)
+            nc.sync.dma_start(out=dst[:, first:last, :], in_=rows[:, first:last, :])
+
+        phase_halves = phase.rearrange("a (g p i) -> p g a i", g=G, i=PACK)
+        nc.scalar.dma_start(out=phase_sb[:, 0:A, 0:PACK], in_=phase_halves[:, 0])
+        load_rows(x_rows[0], x[0:K_PASS, :], 0, 2)
+        load_rows(x_rows[0], x[0:K_PASS, :], 2, 4)
+        load_rows(w_rows[0], w[0])
+        load_rows(w_rows[1], w[1])
+        nc.sync.dma_start(out=phase_sb[:, A : 2 * A, 0:PACK], in_=phase_halves[:, 1])
+        load_rows(x_rows[1], x[K_PASS:T, :])
+        load_rows(w_rows[2], w[2])
+        nc.sync.dma_start(out=v_sb[:, :, 0:PACK], in_=v.rearrange("(g p i) -> p g i", g=G, i=PACK))
+        load_rows(w_rows[3], w[3])
+        load_rows(d_rows[0], d[0:K_PASS, :])
+        load_rows(d_rows[1], d[K_PASS:T, :])
+        nc.sync.dma_start(out=mu_sb[:, :, 0:PACK], in_=mu.rearrange("a (q i) -> q a i", i=PACK))
+
+        ident = kept("ident", [P, P], F32)
+        make_identity(nc, ident[:])
+
+        neg_abs = kept("neg_abs", [P, G * A, PACK], F32)
+        cos_sb = kept("cos_sb", [P, G * A, PACK], F32)
+        v_f32 = kept("v_f32", [P, G, PACK], F32)
+        err_rows = [kept("err_rows%d" % g, [P, PACK, J], BF16) for g in range(G)]
+        err_grouped = [kept("err_grouped%d" % g, [P, J, PACK], BF16) for g in range(G)]
+        result = [kept("result%d" % a, [P, PACK, J], F32) for a in range(A)]
+        plane_codes = kept("plane_codes", [P, A * L], U32)
+        plane_scales = kept("plane_scales", [P, A * L], U8)
+        u_rows, tap_banks, tap_grouped, tap_mx = {}, {}, {}, {}
+        w_grouped, w_mx, est, diff, err_mx = {}, {}, {}, {}, {}
+        time_grouped, time_mx, grad = {}, {}, {}
+        rounded, plane_banks, plane_grouped = {}, {}, {}
+
+        def fold_phase(g):
+            angles = phase_sb[:, A * g : A * (g + 1), 0:PACK]
+            nc.vector.scalar_tensor_tensor(
+                out=neg_abs[:, A * g : A * (g + 1), :], in0=angles, scalar=-1.0, in1=angles, op0=ALU.mult, op1=ALU.min
+            )
+
+        def cosine(g):
+            of_half = slice(A * g, A * (g + 1))
+            nc.scalar.activation(out=cos_sb[:, of_half, :], in_=neg_abs[:, of_half, :], func=ACT.Sin, bias=math.pi / 2)
+
+        def modulate(s):
+            u_rows[s] = kept("u_rows%d" % s, [P, PACK, L], BF16)
+            for i in range(PACK):
+                nc.vector.tensor_scalar(
+                    out=u_rows[s][:, i, :], in0=x_rows[s // A][:, i, :],
+                    scalar1=cos_sb[:, s, i : i + 1], scalar2=None, op0=ALU.mult,
+                )
+
+        def turn_u(s, *pairs):
+            words = u_rows[s][:].rearrange("p i l -> p (i l)").bitcast(F32)
+            for pair in pairs:
+                tap_banks[s, pair] = bank(2 * (s % 2) + pair, "tap_bank%d%d" % (s, pair), [P, 4, P])
+                for n in range(4):
+                    i, h = 2 * pair + n // 2, n % 2
+                    nc.tensor.transpose(tap_banks[s, pair][:, n, :], words[:, HALF * i + h : HALF * (i + 1) : 2], ident[:])
+
+        def gather_taps(s):
+            tap_grouped[s] = staged("tap_grouped", "tap_grouped%d" % s, [P, K_PASS, PACK], BF16)
+            for pair in range(2):
+                cols = tap_grouped[s][:, HALF * pair : HALF * (pair + 1), :]
+                nc.scalar.copy(
+                    out=cols.rearrange("q c k -> q (c k)").bitcast(F32).rearrange("q (i p h) -> q i p h", i=2, h=2),
+                    in_=tap_banks[s, pair][:].rearrange("q (i h) p -> q i p h", h=2),
+                )
+
+        def quantize_taps(s, pair):
+            if pair == 0:
+                codes = staged("tap_codes", "tap_codes%d" % s, [P, K_PASS], U32)
+                scales = staged("tap_scales", "tap_scales%d" % s, [P, K_PASS], U8)
+                tap_mx[s] = codes, scales
+            cols = slice(HALF * pair, HALF * (pair + 1))
+            quantize_columns(tap_mx[s][0][:, cols], tap_mx[s][1][:, cols], tap_grouped[s][:, cols, :])
+
+        def group_w(a):
+            w_grouped[a] = staged("wide_grouped", "w_grouped%d" % a, [P, J, PACK], BF16)
+            group_rows(w_grouped[a], w_rows[a], W_SPLIT[a])
+
+        def quantize_w(a):
+            w_mx[a] = quantize_kept("w%d" % a, w_grouped[a])
+
+        def estimate(s, pair):
+            g, a = divmod(s, A)
+            for i in (2 * pair, 2 * pair + 1):
+                if a == 0:
+                    est[g, i] = bank(EST_BANK + i, "est%d%d" % (g, i), [P, J])
+                mx_pass(est[g, i], tap_mx[s], i, w_mx[a], a == 0, a == A - 1)
+
+        def quantize_and_estimate(s):
+            for pair in range(2):
+                quantize_taps(s, pair)
+                estimate(s, pair)
 
         def weight_error(engine, g, i):
             dst, src, factor = err_rows[g][:, i, :], diff[g][:, i, :], v_f32[:, g, i : i + 1]
-            if engine == "gpsimd":
+            if engine == GPSIMD:
                 nc.gpsimd.tensor_scalar(out=dst, in0=src, scalar1=factor, scalar2=0.0, op0=ALU.mult, op1=ALU.add)
-            elif engine == "vector":
+            elif engine == VECTOR:
                 nc.vector.tensor_scalar(out=dst, in0=src, scalar1=factor, scalar2=None, op0=ALU.mult)
             else:
                 nc.scalar.activation(out=dst, in_=src, func=ACT.Copy, scale=factor)
 
-        def group_err(engine, g, first, last):
-            interleave(engine, err_grouped[g], err_rows[g], first, last)
+        def subtract_estimates(g):
+            diff[g] = keep.tile([P, PACK, J], F32, name="diff%d" % g, tag="diff", align_bytes=64)
+            for i in range(PACK):
+                nc.vector.tensor_tensor(out=diff[g][:, i, :], in0=d_rows[g][:, i, :], in1=est[g, i][:], op=ALU.subtract)
+                if i < 2:
+                    weight_error(GPSIMD, g, i)
 
         def quantize_err(g):
-            err_q[g] = quantize("err_%d" % g, err_grouped[g])
+            err_mx[g] = quantize_kept("err%d" % g, err_grouped[g])
 
-        def group_u2(engine, g, a, u):
-            if (g, a) not in u2_grouped:
-                u2_grouped[g, a] = staged("u2_grouped", "u2_grouped%d%d" % (g, a), [P, L, PACK], BF16)
-            cols = slice(256 * u, 256 * (u + 1))
+        def group_time(engine, s, h):
+            if s not in time_grouped:
+                time_grouped[s] = staged("time_grouped", "time_grouped%d" % s, [P, L, PACK], BF16)
             copy_on(
                 engine,
-                u2_grouped[g, a][:, cols, :].rearrange("p (e c r) i -> p c i r e", e=2, r=2),
-                u_rows[g, a][:, :, cols].rearrange("p i (c r e) -> p c i r e", r=2, e=2) if g in PERM else u_rows[g, a][:].rearrange("p i (c r u e) -> p c i r u e", r=2, u=2, e=2)[:, :, :, :, u, :],
+                time_grouped[s][:, HALF * h : HALF * (h + 1), :].rearrange("p (e c n) i -> p c i n e", e=2, n=2),
+                u_rows[s][:].rearrange("p i (c n h e) -> p c i n h e", n=2, h=2, e=2)[:, :, :, :, h, :],
             )
 
-        def quantize_u2(g, a):
-            u2_q[g, a] = quantize("u2_%d%d" % (g, a), u2_grouped[g, a])
+        def quantize_time(s):
+            time_mx[s] = quantize_kept("time%d" % s, time_grouped[s])
 
-        def gradient(g, a, i):
+        def gradient(g, n):
+            a, i = divmod(n, PACK)
             if g == 0:
-                grad[a, i] = bank((PACK * a + i) % 6, "grad%d%d" % (a, i), [P, J])
-            mx_pass(grad[a, i], u2_q[g, a], i, err_q[g], g == 0, g == G - 1)
+                grad[n] = bank(n % GRAD_BANKS, "grad%d" % n, [P, J])
+            mx_pass(grad[n], time_mx[A * g + a], i, err_mx[g], g == 0, g == G - 1)
 
-        def update(a, i):
+        def update(n, into):
+            a, i = divmod(n, PACK)
             nc.vector.scalar_tensor_tensor(
-                out=result[a][:, i, :], in0=grad[a, i][:], scalar=mu_sb[:, a, i : i + 1], in1=w_rows[a][:, i, :],
+                out=into[a][:, i, :], in0=grad[n][:], scalar=mu_sb[:, a, i : i + 1], in1=w_rows[a][:, i, :],
                 op0=ALU.mult, op1=ALU.add,
             )
 
-        def store_result(a, first, last):
-            nc.sync.dma_start(
-                out=out_0[a].rearrange("(q i) j -> q i j", i=PACK)[:, first:last, :], in_=result[a][:, first:last, :]
-            )
+        def store_result(first, last):
+            a, slots = first // PACK, slice(first % PACK, last % PACK + 1)
+            nc.sync.dma_start(out=out_0[a].rearrange("(q i) j -> q i j", i=PACK)[:, slots, :], in_=result[a][:, slots, :])
 
-        def round_result(engine, a, i):
-            if a not in result_bf:
-                result_bf[a] = staged("result_bf", "result_bf%d" % a, [P, PACK, J], BF16)
-            dst = result_bf[a][:, i, :].rearrange("q (u p e) -> q u p e", u=2, e=2)
-            src = result[a][:, i, :].rearrange("q (p u e) -> q u p e", u=2, e=2)
-            if engine == "gpsimd":
+        def round_result(engine, n):
+            a, i = divmod(n, PACK)
+            if i == 0:
+                rounded[a] = staged("rounded", "rounded%d" % a, [P, PACK, J], BF16)
+            dst = rounded[a][:, i, :].rearrange("q (h r e) -> q h r e", h=2, e=2)
+            src = result[a][:, i, :].rearrange("q (r h e) -> q h r e", h=2, e=2)
+            if engine == GPSIMD:
                 nc.gpsimd.tensor_scalar(out=dst, in0=src, scalar1=1.0, scalar2=0.0, op0=ALU.mult, op1=ALU.add)
             else:
-                copy_on(engine, dst, src)
+                nc.scalar.copy(out=dst, in_=src)
 
-        def update_rounded(a, i):
-            nc.vector.scalar_tensor_tensor(
-                out=result_bf[a][:, i, :], in0=grad[a, i][:], scalar=mu_sb[:, a, i : i + 1], in1=w_rows[a][:, i, :],
-                op0=ALU.mult, op1=ALU.add,
-            )
-
-        def turn_result(a, i, natural=False):
-            half = i // 2
+        def turn_result(n, in_order_of_j=False):
+            a, i = divmod(n, PACK)
             if i % 2 == 0:
-                plane_banks[a, half] = bank((6 if a < A - 1 else 4) + half, "plane_bank%d%d" % (a, half), [P, 4, P])
-            words = result_bf[a][:, i, :].bitcast(F32)
-            for u in range(2):
-                src = words[:, u:256:2] if natural else words[:, u * P : (u + 1) * P]
-                nc.tensor.transpose(plane_banks[a, half][:, 2 * (i % 2) + u, :], src, ident[:])
+                number = (PLANE_BANK if a < A - 1 else LAST_PLANE_BANK) + i // 2
+                plane_banks[n // 2] = bank(number, "plane_bank%d" % (n // 2), [P, 4, P])
+            words = rounded[a][:, i, :].bitcast(F32)
+            for h in range(2):
+                src = words[:, h:HALF:2] if in_order_of_j else words[:, h * P : (h + 1) * P]
+                nc.tensor.transpose(plane_banks[n // 2][:, 2 * (i % 2) + h, :], src, ident[:])
 
-        def gather_plane(engine, a, half, first=0, last=P):
-            if a not in plane_grouped:
-                plane_grouped[a] = staged("plane_grouped", "plane_grouped%d" % a, [P, L, PACK], BF16)
-            words = plane_grouped[a][:].rearrange("p m k -> p (m k)").bitcast(F32)
-            copy_on(
-                engine,
-                words.rearrange("p (q i u) -> p q i u", i=PACK, u=2)[:, first:last, 2 * half : 2 * half + 2, :],
-                plane_banks[a, half][:].rearrange("p (i u) q -> p q i u", u=2)[:, first:last],
+        def gather_plane(tile_pair, first=0, last=P):
+            a, pair = divmod(tile_pair, 2)
+            if pair == 0:
+                plane_grouped[a] = staged("wide_grouped", "plane_grouped%d" % a, [P, L, PACK], BF16)
+            words = plane_grouped[a][:].rearrange("r l k -> r (l k)").bitcast(F32)
+            nc.scalar.copy(
+                out=words.rearrange("r (q i h) -> r q i h", i=PACK, h=2)[:, first:last, 2 * pair : 2 * pair + 2, :],
+                in_=plane_banks[tile_pair][:].rearrange("r (i h) q -> r q i h", h=2)[:, first:last],
             )
 
         def quantize_plane(a, first=0, last=L):
             cols = slice(a * L + first, a * L + last)
-            nc.vector.quantize_mx(
-                out=plane_codes[:, cols].bitcast(FP8X4), scales=plane_scales[:, cols],
-                in_=plane_grouped[a][:, first:last, :].rearrange("p m k -> p (m k)"),
-            )
-            words = out_1.rearrange("g p m k -> (g p) (m k)").bitcast(I32)
+            quantize_columns(plane_codes[:, cols], plane_scales[:, cols], plane_grouped[a][:, first:last, :])
+            words = out_1.rearrange("g r m k -> (g r) (m k)").bitcast(I32)
             nc.sync.dma_start(out=words[:, cols], in_=plane_codes[:, cols].bitcast(I32))
 
         def store_scales():
-            for quad in range(4):
-                queue = nc.sync if quad % 2 == 0 else nc.scalar
+            for quadrant in range(4):
+                queue = nc.sync if quadrant % 2 == 0 else nc.scalar
                 queue.dma_start(
-                    out=out_2[0, 4 * quad : 4 * quad + 4, :].bitcast(I32),
-                    in_=plane_scales[32 * quad : 32 * quad + 4, :].bitcast(I32),
+                    out=out_2[0, 4 * quadrant : 4 * quadrant + 4, :].bitcast(I32),
+                    in_=plane_scales[32 * quadrant : 32 * quadrant + 4, :].bitcast(I32),
                 )
-
-        PERM = (1,)
-        V, S, Q = "vector", "scalar", "gpsimd"
-        steps = [(g, a) for g in range(G) for a in range(A)]
-
-        def modulate_and_turn(k):
-            modulate(*steps[k])
-            turn_u(*steps[k], 0)
-            turn_u(*steps[k], 1)
-
-        def gather(k):
-            gather_u1(S, *steps[k], 0)
-            gather_u1(S, *steps[k], 1)
-
-        def stage_one(k):
-            for half in range(2):
-                quantize_u1(*steps[k], half)
-                estimate(*steps[k], half)
 
         fold_phase(0)
         cosine(0)
-        modulate_and_turn(0)
-        group_u2(S, 0, 0, 0)
-        modulate_and_turn(1)
-        modulate(*steps[2])
-        group_w(V, 0, 0, 512)
-        gather(0)
-        turn_u(*steps[2], 0)
-        turn_u(*steps[2], 1)
-        modulate(*steps[3])
-        group_u2(S, 0, 0, 1)
+        modulate(0)
+        turn_u(0, 0, 1)
+        group_time(SCALAR, 0, 0)
+        modulate(1)
+        turn_u(1, 0, 1)
+        modulate(2)
+        group_w(0)
+        gather_taps(0)
+        turn_u(2, 0, 1)
+        modulate(3)
+        group_time(SCALAR, 0, 1)
         fold_phase(1)
-        permute_x(V, 1, 0, 4)
         quantize_w(0)
-        group_w(V, 1, 0, 512)
-        stage_one(0)
+        group_w(1)
+        quantize_and_estimate(0)
         cosine(1)
-        gather(1)
-        turn_u(*steps[3], 0)
-        turn_u(*steps[3], 1)
-        group_w(S, 2, 192, 512)
+        gather_taps(1)
+        turn_u(3, 0, 1)
         quantize_w(1)
-        group_w(V, 2, 0, 192)
-        modulate(*steps[4])
-        stage_one(1)
-        gather(2)
-        turn_u(*steps[4], 0)
-        turn_u(*steps[4], 1)
-        group_w(S, 3, 0, 512)
-        quantize_u2(0, 0)
+        group_w(2)
+        modulate(4)
+        quantize_and_estimate(1)
+        gather_taps(2)
+        turn_u(4, 0, 1)
+        group_w(3)
+        quantize_time(0)
         quantize_w(2)
-        modulate(*steps[5])
-        stage_one(2)
-        gather(3)
-        turn_u(*steps[5], 0)
-        turn_u(*steps[5], 1)
-        group_u2(S, 1, 0, 0)
-        modulate(*steps[6])
-        group_u2(V, 0, 1, 0)
+        modulate(5)
+        quantize_and_estimate(2)
+        gather_taps(3)
+        turn_u(5, 0, 1)
+        group_time(SCALAR, 4, 0)
+        modulate(6)
+        group_time(VECTOR, 1, 0)
         quantize_w(3)
-        stage_one(3)
-        gather(4)
-        turn_u(*steps[6], 0)
-        turn_u(*steps[6], 1)
-        group_u2(S, 1, 0, 1)
-        modulate(*steps[7])
-        group_u2(V, 0, 1, 1)
-        widen_v()
-        quantize_u1(*steps[4], 0)
-        quantize_u1(*steps[4], 1)
-        gather(5)
-        turn_u(*steps[7], 0)
-        turn_u(*steps[7], 1)
-        group_u2(S, 1, 1, 0)
-        quantize_u2(0, 1)
-        for i in range(PACK):
-            subtract_estimate(0, i)
-            if i < 2:
-                weight_error(Q, 0, i)
-        estimate(*steps[4], 0)
-        estimate(*steps[4], 1)
-        gather(6)
-        stage_one(5)
-        weight_error(S, 0, 2)
-        weight_error(S, 0, 3)
-        gather(7)
-        quantize_u2(1, 0)
-        stage_one(6)
-        group_u2(V, 1, 1, 1)
-        stage_one(7)
-        group_err(S, 0, 0, 512)
-        group_u2(S, 0, 2, 0)
-        quantize_u2(1, 1)
-        for i in range(PACK):
-            subtract_estimate(1, i)
-            if i < 2:
-                weight_error(Q, 1, i)
-        group_u2(S, 0, 2, 1)
-        weight_error(V, 1, 2)
-        weight_error(V, 1, 3)
+        quantize_and_estimate(3)
+
+        gather_taps(4)
+        turn_u(6, 0, 1)
+        group_time(SCALAR, 4, 1)
+        modulate(7)
+        group_time(VECTOR, 1, 1)
+        nc.vector.tensor_copy(out=v_f32[:], in_=v_sb[:, :, 0:PACK])
+        quantize_taps(4, 0)
+        quantize_taps(4, 1)
+        gather_taps(5)
+        turn_u(7, 0)
+        group_time(SCALAR, 5, 0)
+        quantize_time(1)
+        subtract_estimates(0)
+        estimate(4, 0)
+        turn_u(7, 1)
+        estimate(4, 1)
+        gather_taps(6)
+        quantize_and_estimate(5)
+        weight_error(SCALAR, 0, 2)
+        weight_error(SCALAR, 0, 3)
+        gather_taps(7)
+        quantize_time(4)
+        quantize_and_estimate(6)
+        group_time(VECTOR, 5, 1)
+        quantize_and_estimate(7)
+        group_rows(err_grouped[0], err_rows[0], ERR_SPLIT[0])
+        group_time(SCALAR, 2, 0)
+        quantize_time(5)
+
+        subtract_estimates(1)
+        group_time(SCALAR, 2, 1)
+        weight_error(VECTOR, 1, 2)
+        weight_error(VECTOR, 1, 3)
         quantize_err(0)
-        for n in range(4):
-            gradient(0, n // PACK, n % PACK)
-        group_err(S, 1, 288, 512)
-        group_err(V, 1, 0, 288)
-        group_u2(V, 1, 2, 0)
-        group_u2(S, 1, 2, 1)
+        for n in range(PACK):
+            gradient(0, n)
+        group_rows(err_grouped[1], err_rows[1], ERR_SPLIT[1])
+        group_time(VECTOR, 6, 0)
+        group_time(SCALAR, 6, 1)
         quantize_err(1)
-        for n in range(4):
-            gradient(1, n // PACK, n % PACK)
-        for n in range(4, 6):
-            gradient(0, n // PACK, n % PACK)
-            gradient(1, n // PACK, n % PACK)
-        quantize_u2(0, 2)
-        quantize_u2(1, 2)
-        for g in range(G):
-            group_u2(S, g, 3, 0)
-            group_u2(S, g, 3, 1)
-        tiles = [(a, i) for a in range(A) for i in range(PACK)]
-        rounder = [Q, Q, Q, Q, S, Q, Q, Q, S, S, S, Q, Q, S, S]
-        turn_after = {2: 0, 4: 1, 7: 2, 9: 3, 10: 4, 12: 5, 14: 6}
-        gather_after = {4: 0, 5: 1, 8: 2, 9: 3, 11: 4, 14: 5}
-        gradients_after = {1: (6, 7), 3: (8, 9), 5: (10, 11), 10: (12, 13, 14), 11: (15,)}
-        last = len(tiles) - 1
+        for n in range(PACK):
+            gradient(1, n)
+        for n in range(PACK, GRAD_BANKS):
+            gradient(0, n)
+            gradient(1, n)
+        quantize_time(2)
+        quantize_time(6)
+        for s in (3, 7):
+            group_time(SCALAR, s, 0)
+            group_time(SCALAR, s, 1)
+
+        last = A * PACK - 1
+        end_of_first_run = 10
+        rounded_by_gpsimd = (0, 1, 2, 3, 5, 6, 7, 11, 12)
+        gradient_pair_after = {1: 3, 3: 4, 5: 5, 10: 6, 11: 7}
+        turn_pair_after = {2: 0, 4: 1, 7: 2, 9: 3, 10: 4, 12: 5, 14: 6}
+        gather_pair_after = {4: 0, 5: 1, 8: 2, 9: 3, 11: 4, 14: 5}
         for n in range(last):
-            a, i = tiles[n]
-            update(a, i)
-            if i % 2 == 1:
-                store_result(a, i - 1, i + 1)
-            if n == 10:
-                quantize_u2(0, 3)
-                quantize_u2(1, 3)
+            update(n, result)
+            if n % 2 == 1:
+                store_result(n - 1, n)
+            if n == end_of_first_run:
+                quantize_time(3)
+                quantize_time(7)
                 quantize_plane(0)
-            if n < last:
-                round_result(rounder[n], a, i)
-            if n in gradients_after:
-                for t in gradients_after[n]:
-                    gradient(0, *tiles[t])
-                    gradient(1, *tiles[t])
-            if n in turn_after:
-                pair = turn_after[n]
-                turn_result(*tiles[2 * pair])
-                turn_result(*tiles[2 * pair + 1])
-            if n in gather_after:
-                gather_plane(S, gather_after[n] // 2, gather_after[n] % 2)
-        store_result(3, 2, 3)
-        update_rounded(3, 3)
+            round_result(GPSIMD if n in rounded_by_gpsimd else SCALAR, n)
+            if n in gradient_pair_after:
+                for m in (2 * gradient_pair_after[n], 2 * gradient_pair_after[n] + 1):
+                    gradient(0, m)
+                    gradient(1, m)
+            if n in turn_pair_after:
+                turn_result(2 * turn_pair_after[n])
+                turn_result(2 * turn_pair_after[n] + 1)
+            if n in gather_pair_after:
+                gather_plane(gather_pair_after[n])
+
+        store_result(last - 1, last - 1)
+        update(last, rounded)
         quantize_plane(1)
-        turn_result(3, 2)
-        turn_result(3, 3, natural=True)
-        gather_plane(S, 3, 0)
-        update(3, 3)
-        store_result(3, 3, 4)
+        turn_result(last - 1)
+        turn_result(last, in_order_of_j=True)
+        gather_plane(last // 2 - 1)
+        update(last, result)
+        store_result(last, last)
         quantize_plane(2)
-        gather_plane(S, 3, 1, 0, 64)
-        gather_plane(S, 3, 1, 64, 128)
-        quantize_plane(3, 0, 256)
-        quantize_plane(3, 256, 512)
+        gather_plane(last // 2, 0, P // 2)
+        gather_plane(last // 2, P // 2, P)
+        quantize_plane(A - 1, 0, HALF)
+        quantize_plane(A - 1, HALF, L)
         store_scales()

import math
from contextlib import ExitStack

import concourse.mybir as mybir
from concourse.masks import make_identity

A, T, L, J = 4, 1024, 512, 512
FLOPS = 2 * 2 * T * A * L * J

F32 = mybir.dt.float32
BF16 = mybir.dt.bfloat16
U32 = mybir.dt.uint32
I32 = mybir.dt.int32
U8 = mybir.dt.uint8
FP8X4 = mybir.dt.float8_e4m3fn_x4
ALU = mybir.AluOpType
ACT = mybir.ActivationFunctionType

P = 128
PACK = 4
K_PASS = P * PACK
G = T // K_PASS
HALF = K_PASS // 2
PITCH = 16
RUN = 4

EST_BANK, GRAD_BANKS, PLANE_BANK, LAST_PLANE_BANK = 4, 6, 6, 4

VECTOR, SCALAR, GPSIMD = "vector", "scalar", "gpsimd"

W_SPLIT = (J, J, 192, 0)
ERR_SPLIT = (96, 256)


def tile_freshcyclicfilterblocklmsupdate_x1_kernel(tc, x, d, w, phase, v, mu, out_0, out_1, out_2):
    nc = tc.nc
    with ExitStack() as ctx:
        keep = ctx.enter_context(tc.tile_pool(name="keep", bufs=1))
        stage = ctx.enter_context(tc.tile_pool(name="stage", bufs=3))
        psum = ctx.enter_context(tc.psum_pool(name="psum", bufs=1))
        ctx.enter_context(tc.manual_schedule())

        def kept(name, shape, dtype):
            return keep.tile(shape, dtype, name=name, align_bytes=64)

        def staged(tag, name, shape, dtype):
            return stage.tile(shape, dtype, name=name, tag=tag, align_bytes=64)

        def bank(number, name, shape):
            return psum.tile(shape, F32, name=name, tag="bank%d" % number)

        def copy_on(engine, out, in_):
            if engine == VECTOR:
                nc.vector.tensor_copy(out=out, in_=in_)
            else:
                nc.scalar.copy(out=out, in_=in_)

        def quantize_columns(codes, scales, grouped):
            nc.vector.quantize_mx(out=codes.bitcast(FP8X4), scales=scales, in_=grouped.rearrange("p c i -> p (c i)"))

        def quantize_kept(name, grouped):
            codes = kept(name + "_codes", [P, K_PASS], U32)
            scales = kept(name + "_scales", [P, K_PASS], U8)
            quantize_columns(codes[:], scales[:], grouped[:])
            return codes, scales

        def group_rows(grouped, rows, split):
            for engine, first, last in ((SCALAR, split, K_PASS), (VECTOR, 0, split)):
                if first < last:
                    copy_on(
                        engine,
                        grouped[:, first:last, :].rearrange("p (c n) i -> p c i n", n=RUN),
                        rows[:, :, first:last].rearrange("p i (c n) -> p c i n", n=RUN),
                    )

        def mx_pass(acc, stationary, i, moving, start, stop):
            cols = slice(i * P, (i + 1) * P)
            nc.tensor.matmul_mx(
                out=acc[:], lhsT=stationary[0][:, cols].bitcast(FP8X4), lhsT_scale=stationary[1][:, cols],
                rhs=moving[0][:].bitcast(FP8X4), rhs_scale=moving[1][:], start=start, stop=stop,
            )

        phase_sb = kept("phase_sb", [P, G * A, PITCH], BF16)
        v_sb = kept("v_sb", [P, G, PITCH], BF16)
        mu_sb = kept("mu_sb", [P, A, PITCH], BF16)
        x_rows = [kept("x_rows%d" % g, [P, PACK, L], BF16) for g in range(G)]
        d_rows = [kept("d_rows%d" % g, [P, PACK, J], BF16) for g in range(G)]
        w_rows = [kept("w_rows%d" % a, [P, PACK, J], BF16) for a in range(A)]

        def load_rows(dst, src, first=0, last=PACK):
            rows = src.rearrange("(p i) c -> p i c", i=PACK)
            nc.sync.dma_start(out=dst[:, first:last, :], in_=rows[:, first:last, :])

        phase_halves = phase.rearrange("a (g p i) -> p g a i", g=G, i=PACK)
        nc.scalar.dma_start(out=phase_sb[:, 0:A, 0:PACK], in_=phase_halves[:, 0])
        load_rows(x_rows[0], x[0:K_PASS, :], 0, 2)
        load_rows(x_rows[0], x[0:K_PASS, :], 2, 4)
        load_rows(w_rows[0], w[0])
        load_rows(w_rows[1], w[1])
        nc.sync.dma_start(out=phase_sb[:, A : 2 * A, 0:PACK], in_=phase_halves[:, 1])
        load_rows(x_rows[1], x[K_PASS:T, :])
        load_rows(w_rows[2], w[2])
        nc.sync.dma_start(out=v_sb[:, :, 0:PACK], in_=v.rearrange("(g p i) -> p g i", g=G, i=PACK))
        load_rows(w_rows[3], w[3])
        load_rows(d_rows[0], d[0:K_PASS, :])
        load_rows(d_rows[1], d[K_PASS:T, :])
        nc.sync.dma_start(out=mu_sb[:, :, 0:PACK], in_=mu.rearrange("a (q i) -> q a i", i=PACK))

        ident = kept("ident", [P, P], F32)
        make_identity(nc, ident[:])

        neg_abs = kept("neg_abs", [P, G * A, PACK], F32)
        cos_sb = kept("cos_sb", [P, G * A, PACK], F32)
        v_f32 = kept("v_f32", [P, G, PACK], F32)
        err_rows = [kept("err_rows%d" % g, [P, PACK, J], BF16) for g in range(G)]
        err_grouped = [kept("err_grouped%d" % g, [P, J, PACK], BF16) for g in range(G)]
        result = [kept("result%d" % a, [P, PACK, J], F32) for a in range(A)]
        plane_codes = kept("plane_codes", [P, A * L], U32)
        plane_scales = kept("plane_scales", [P, A * L], U8)
        u_rows, tap_banks, tap_grouped, tap_mx = {}, {}, {}, {}
        w_grouped, w_mx, est, diff, err_mx = {}, {}, {}, {}, {}
        time_grouped, time_mx, grad = {}, {}, {}
        rounded, plane_banks, plane_grouped = {}, {}, {}

        def fold_phase(g):
            angles = phase_sb[:, A * g : A * (g + 1), 0:PACK]
            nc.vector.scalar_tensor_tensor(
                out=neg_abs[:, A * g : A * (g + 1), :], in0=angles, scalar=-1.0, in1=angles, op0=ALU.mult, op1=ALU.min
            )

        def cosine(g):
            of_half = slice(A * g, A * (g + 1))
            nc.scalar.activation(out=cos_sb[:, of_half, :], in_=neg_abs[:, of_half, :], func=ACT.Sin, bias=math.pi / 2)

        def modulate(s):
            u_rows[s] = kept("u_rows%d" % s, [P, PACK, L], BF16)
            for i in range(PACK):
                nc.vector.tensor_scalar(
                    out=u_rows[s][:, i, :], in0=x_rows[s // A][:, i, :],
                    scalar1=cos_sb[:, s, i : i + 1], scalar2=None, op0=ALU.mult,
                )

        def turn_u(s, *pairs):
            words = u_rows[s][:].rearrange("p i l -> p (i l)").bitcast(F32)
            for pair in pairs:
                tap_banks[s, pair] = bank(2 * (s % 2) + pair, "tap_bank%d%d" % (s, pair), [P, 4, P])
                for n in range(4):
                    i, h = 2 * pair + n // 2, n % 2
                    nc.tensor.transpose(tap_banks[s, pair][:, n, :], words[:, HALF * i + h : HALF * (i + 1) : 2], ident[:])

        def gather_taps(s):
            tap_grouped[s] = staged("tap_grouped", "tap_grouped%d" % s, [P, K_PASS, PACK], BF16)
            for pair in range(2):
                cols = tap_grouped[s][:, HALF * pair : HALF * (pair + 1), :]
                nc.scalar.copy(
                    out=cols.rearrange("q c k -> q (c k)").bitcast(F32).rearrange("q (i p h) -> q i p h", i=2, h=2),
                    in_=tap_banks[s, pair][:].rearrange("q (i h) p -> q i p h", h=2),
                )

        def quantize_taps(s, pair):
            if pair == 0:
                codes = staged("tap_codes", "tap_codes%d" % s, [P, K_PASS], U32)
                scales = staged("tap_scales", "tap_scales%d" % s, [P, K_PASS], U8)
                tap_mx[s] = codes, scales
            cols = slice(HALF * pair, HALF * (pair + 1))
            quantize_columns(tap_mx[s][0][:, cols], tap_mx[s][1][:, cols], tap_grouped[s][:, cols, :])

        def group_w(a):
            w_grouped[a] = staged("wide_grouped", "w_grouped%d" % a, [P, J, PACK], BF16)
            group_rows(w_grouped[a], w_rows[a], W_SPLIT[a])

        def quantize_w(a):
            w_mx[a] = quantize_kept("w%d" % a, w_grouped[a])

        def estimate(s, pair):
            g, a = divmod(s, A)
            for i in (2 * pair, 2 * pair + 1):
                if a == 0:
                    est[g, i] = bank(EST_BANK + i, "est%d%d" % (g, i), [P, J])
                mx_pass(est[g, i], tap_mx[s], i, w_mx[a], a == 0, a == A - 1)

        def quantize_and_estimate(s):
            for pair in range(2):
                quantize_taps(s, pair)
                estimate(s, pair)

        def weight_error(engine, g, i):
            dst, src, factor = err_rows[g][:, i, :], diff[g][:, i, :], v_f32[:, g, i : i + 1]
            if engine == GPSIMD:
                nc.gpsimd.tensor_scalar(out=dst, in0=src, scalar1=factor, scalar2=0.0, op0=ALU.mult, op1=ALU.add)
            elif engine == VECTOR:
                nc.vector.tensor_scalar(out=dst, in0=src, scalar1=factor, scalar2=None, op0=ALU.mult)
            else:
                nc.scalar.activation(out=dst, in_=src, func=ACT.Copy, scale=factor)

        def subtract_estimates(g):
            diff[g] = keep.tile([P, PACK, J], F32, name="diff%d" % g, tag="diff", align_bytes=64)
            for i in range(PACK):
                nc.vector.tensor_tensor(out=diff[g][:, i, :], in0=d_rows[g][:, i, :], in1=est[g, i][:], op=ALU.subtract)
                if i < 2:
                    weight_error(GPSIMD, g, i)

        def quantize_err(g):
            err_mx[g] = quantize_kept("err%d" % g, err_grouped[g])

        def group_time(engine, s, h):
            if s not in time_grouped:
                time_grouped[s] = staged("time_grouped", "time_grouped%d" % s, [P, L, PACK], BF16)
            copy_on(
                engine,
                time_grouped[s][:, HALF * h : HALF * (h + 1), :].rearrange("p (e c n) i -> p c i n e", e=2, n=2),
                u_rows[s][:].rearrange("p i (c n h e) -> p c i n h e", n=2, h=2, e=2)[:, :, :, :, h, :],
            )

        def quantize_time(s):
            time_mx[s] = quantize_kept("time%d" % s, time_grouped[s])

        def gradient(g, n):
            a, i = divmod(n, PACK)
            if g == 0:
                grad[n] = bank(n % GRAD_BANKS, "grad%d" % n, [P, J])
            mx_pass(grad[n], time_mx[A * g + a], i, err_mx[g], g == 0, g == G - 1)

        def update(n, into):
            a, i = divmod(n, PACK)
            nc.vector.scalar_tensor_tensor(
                out=into[a][:, i, :], in0=grad[n][:], scalar=mu_sb[:, a, i : i + 1], in1=w_rows[a][:, i, :],
                op0=ALU.mult, op1=ALU.add,
            )

        def store_result(first, last):
            a, slots = first // PACK, slice(first % PACK, last % PACK + 1)
            nc.sync.dma_start(out=out_0[a].rearrange("(q i) j -> q i j", i=PACK)[:, slots, :], in_=result[a][:, slots, :])

        def round_result(engine, n):
            a, i = divmod(n, PACK)
            if i == 0:
                rounded[a] = staged("rounded", "rounded%d" % a, [P, PACK, J], BF16)
            dst = rounded[a][:, i, :].rearrange("q (h r e) -> q h r e", h=2, e=2)
            src = result[a][:, i, :].rearrange("q (r h e) -> q h r e", h=2, e=2)
            if engine == GPSIMD:
                nc.gpsimd.tensor_scalar(out=dst, in0=src, scalar1=1.0, scalar2=0.0, op0=ALU.mult, op1=ALU.add)
            else:
                nc.scalar.copy(out=dst, in_=src)

        def turn_result(n, in_order_of_j=False):
            a, i = divmod(n, PACK)
            if i % 2 == 0:
                number = (PLANE_BANK if a < A - 1 else LAST_PLANE_BANK) + i // 2
                plane_banks[n // 2] = bank(number, "plane_bank%d" % (n // 2), [P, 4, P])
            words = rounded[a][:, i, :].bitcast(F32)
            for h in range(2):
                src = words[:, h:HALF:2] if in_order_of_j else words[:, h * P : (h + 1) * P]
                nc.tensor.transpose(plane_banks[n // 2][:, 2 * (i % 2) + h, :], src, ident[:])

        def gather_plane(tile_pair, first=0, last=P):
            a, pair = divmod(tile_pair, 2)
            if pair == 0:
                plane_grouped[a] = staged("wide_grouped", "plane_grouped%d" % a, [P, L, PACK], BF16)
            words = plane_grouped[a][:].rearrange("r l k -> r (l k)").bitcast(F32)
            nc.scalar.copy(
                out=words.rearrange("r (q i h) -> r q i h", i=PACK, h=2)[:, first:last, 2 * pair : 2 * pair + 2, :],
                in_=plane_banks[tile_pair][:].rearrange("r (i h) q -> r q i h", h=2)[:, first:last],
            )

        def quantize_plane(a, first=0, last=L):
            cols = slice(a * L + first, a * L + last)
            quantize_columns(plane_codes[:, cols], plane_scales[:, cols], plane_grouped[a][:, first:last, :])
            words = out_1.rearrange("g r m k -> (g r) (m k)").bitcast(I32)
            nc.sync.dma_start(out=words[:, cols], in_=plane_codes[:, cols].bitcast(I32))

        def store_scales():
            for quadrant in range(4):
                queue = nc.sync if quadrant % 2 == 0 else nc.scalar
                queue.dma_start(
                    out=out_2[0, 4 * quadrant : 4 * quadrant + 4, :].bitcast(I32),
                    in_=plane_scales[32 * quadrant : 32 * quadrant + 4, :].bitcast(I32),
                )

        fold_phase(0)
        cosine(0)
        modulate(0)
        turn_u(0, 0, 1)
        group_time(SCALAR, 0, 0)
        modulate(1)
        turn_u(1, 0, 1)
        modulate(2)
        group_w(0)
        gather_taps(0)
        turn_u(2, 0, 1)
        modulate(3)
        group_time(SCALAR, 0, 1)
        fold_phase(1)
        quantize_w(0)
        group_w(1)
        quantize_and_estimate(0)
        cosine(1)
        gather_taps(1)
        turn_u(3, 0, 1)
        quantize_w(1)
        group_w(2)
        modulate(4)
        quantize_and_estimate(1)
        gather_taps(2)
        turn_u(4, 0, 1)
        group_w(3)
        quantize_time(0)
        quantize_w(2)
        modulate(5)
        quantize_and_estimate(2)
        gather_taps(3)
        turn_u(5, 0, 1)
        group_time(SCALAR, 4, 0)
        modulate(6)
        group_time(VECTOR, 1, 0)
        quantize_w(3)
        quantize_and_estimate(3)

        gather_taps(4)
        turn_u(6, 0, 1)
        group_time(SCALAR, 4, 1)
        modulate(7)
        group_time(VECTOR, 1, 1)
        nc.vector.tensor_copy(out=v_f32[:], in_=v_sb[:, :, 0:PACK])
        quantize_taps(4, 0)
        quantize_taps(4, 1)
        gather_taps(5)
        turn_u(7, 0)
        group_time(SCALAR, 5, 0)
        quantize_time(1)
        subtract_estimates(0)
        estimate(4, 0)
        turn_u(7, 1)
        estimate(4, 1)
        gather_taps(6)
        quantize_and_estimate(5)
        weight_error(SCALAR, 0, 2)
        weight_error(SCALAR, 0, 3)
        gather_taps(7)
        quantize_time(4)
        quantize_and_estimate(6)
        group_time(VECTOR, 5, 1)
        quantize_and_estimate(7)
        group_rows(err_grouped[0], err_rows[0], ERR_SPLIT[0])
        group_time(SCALAR, 2, 0)
        quantize_time(5)

        subtract_estimates(1)
        group_time(SCALAR, 2, 1)
        weight_error(VECTOR, 1, 2)
        weight_error(VECTOR, 1, 3)
        quantize_err(0)
        for n in range(PACK):
            gradient(0, n)
        group_rows(err_grouped[1], err_rows[1], ERR_SPLIT[1])
        group_time(VECTOR, 6, 0)
        group_time(SCALAR, 6, 1)
        quantize_err(1)
        for n in range(PACK):
            gradient(1, n)
        for n in range(PACK, GRAD_BANKS):
            gradient(0, n)
            gradient(1, n)
        quantize_time(2)
        quantize_time(6)
        for s in (3, 7):
            group_time(SCALAR, s, 0)
            group_time(SCALAR, s, 1)

        last = A * PACK - 1
        end_of_first_run = 10
        rounded_by_gpsimd = (0, 1, 2, 3, 5, 6, 7, 11, 12)
        gradient_pair_after = {1: 3, 3: 4, 5: 5, 10: 6, 11: 7}
        turn_pair_after = {2: 0, 4: 1, 7: 2, 9: 3, 10: 4, 12: 5, 14: 6}
        gather_pair_after = {4: 0, 5: 1, 8: 2, 9: 3, 11: 4, 14: 5}
        for n in range(last):
            update(n, result)
            if n % 2 == 1:
                store_result(n - 1, n)
            if n == end_of_first_run:
                quantize_time(3)
                quantize_time(7)
                quantize_plane(0)
            round_result(GPSIMD if n in rounded_by_gpsimd else SCALAR, n)
            if n in gradient_pair_after:
                for m in (2 * gradient_pair_after[n], 2 * gradient_pair_after[n] + 1):
                    gradient(0, m)
                    gradient(1, m)
            if n in turn_pair_after:
                turn_result(2 * turn_pair_after[n])
                turn_result(2 * turn_pair_after[n] + 1)
            if n in gather_pair_after:
                gather_plane(gather_pair_after[n])

        store_result(last - 1, last - 1)
        update(last, rounded)
        quantize_plane(1)
        turn_result(last - 1)
        turn_result(last, in_order_of_j=True)
        gather_plane(last // 2 - 1)
        update(last, result)
        store_result(last, last)
        quantize_plane(2)
        gather_plane(last // 2, 0, P // 2)
        gather_plane(last // 2, P // 2, P)
        quantize_plane(A - 1, 0, HALF)
        quantize_plane(A - 1, HALF, L)
        store_scales()
